import numpy as np, ml_dtypes
CORES = [36,164,52,180,100,228,116,244]
N = 8
BF = ml_dtypes.bfloat16
def gentries(a):
    return np.ascontiguousarray(a.reshape(8, 16, -1).transpose(0, 2, 1)).reshape(8, -1)
def gtable(e):
    e = np.asarray(e); return np.ascontiguousarray(e.reshape(8, -1, 16).transpose(0, 2, 1)).reshape(128, -1).astype(np.int32)
V, RO, SH = 384, 3, 2
W = N * V
E = 16 * W
def join(ro, a, b):
    ro[a] = b; ro[b] = a
def couple(rng, ro, q):
    q = rng.permutation(q); h = len(q) // 2
    join(ro, q[:h], q[h:2 * h])
    if len(q) > 2 * h: ro[q[-1]] = q[-1]
def rest(rng, ro):
    couple(rng, ro, np.flatnonzero(ro < 0))
def pack(ro, X):
    x = np.ascontiguousarray(X.reshape(8, N, V, 16).transpose(1, 0, 3, 2)).reshape(N, 128, V)
    return {"rot": np.stack([gtable(ro[:, 16 * V * r:16 * V * (r + 1)]) for r in range(N)]), "x": x.astype(np.float32).astype(BF)}
def parities(rng, mode):
    par = np.zeros((8, N, V), np.int64)
    for r in range(N):
        c = int(mode[r])
        if c == 4: par[:, r] = rng.integers(0, 2, (8, V))
        if c in (1, 2): par[:, r] = 1
        if c in (2, 3): par[int(rng.integers(0, 8)), r, int(rng.integers(0, V))] ^= 1
    return par.reshape(8, W)
def voted(rng, ro, h, par, one):
    s = np.argsort(rng.random((W, 8)), axis=1)[:, :2]
    if one: s = np.full((W, 1), int(rng.integers(0, 8)))
    c = np.zeros((W, 16), bool); np.put_along_axis(c, 2 * s + par[:, None], True, 1); c = c.reshape(-1)
    free = ro < 0; hh = np.repeat(h, 16)
    join(ro, rng.permutation(np.flatnonzero(free & c & hh)), rng.permutation(np.flatnonzero(free & c & ~hh)))
    couple(rng, ro, np.flatnonzero(free & ~c & hh)); couple(rng, ro, np.flatnonzero(free & ~c & ~hh))
def nearly(rng, ro, X):
    q = np.concatenate([np.array([W - 1, 0]), 1 + rng.permutation(W - 2)[:10]])
    for b in range(4):
        i, j = sorted(int(v) for v in rng.permutation(16)[:2])
        if b & 1: i, j = j, i
        w, u, z = int(q[b]), int(q[4 + 2 * b]), int(q[5 + 2 * b]); e = 255 * int(rng.integers(0, 2))
        X[w] = e; X[u] = 255 - e; X[z] = 255 - e; X[u, int(rng.integers(0, 16))] = abs(254 - e)
        join(ro, 16 * w + i, 16 * u + int(rng.integers(0, 16))); join(ro, 16 * w + j, 16 * z + int(rng.integers(0, 16)))
def setup_inputs(rng):
    ro = np.full((8, E), -1, np.int64); X = rng.integers(0, 256, (8, W, 16))
    s = rng.integers(0, 32, (8, 8, 16)); pal = np.where(rng.random(s.shape) < 0.5, s, 255 - s)
    X = np.where(rng.random((8, W, 1)) < 0.25, pal[np.arange(8)[:, None], rng.integers(0, 8, (8, W))], X)
    for g in range(8):
        q = rng.permutation(E)[:32]; ro[g, q] = q
        rest(rng, ro[g])
    return pack(ro, X)
def setup_inputs_spread(rng):
    ro = np.full((8, E), -1, np.int64)
    X = np.minimum((np.exp2(9 * rng.random((8, W, 1)) - 2 * rng.random((8, 1, 16))) * rng.random((8, W, 16))).astype(np.int64), 255)
    share = rng.permutation(np.array([0.0, 0.1, 0.3, 0.5, 0.7, 0.8, 0.9, 0.97])); q = rng.permutation(N)
    for g in range(8):
        join(ro[g], 16 * V * int(q[0]) + rng.permutation(16 * V), 16 * V * int(q[1]) + rng.permutation(16 * V))
        for r in q[2:]:
            couple(rng, ro[g], 16 * V * int(r) + np.flatnonzero(rng.random(16 * V) < share[g]))
        rest(rng, ro[g])
    return pack(ro, X)
def setup_inputs_ends(rng):
    ro = np.full((8, E), -1, np.int64); mode = np.full(N, 4); mode[:3] = (0, 2, 3); mode[N - 1] = 1
    par = parities(rng, mode); X = np.zeros((8, W, 16), np.int64); z = 16 * (W - 1)
    for g in range(8):
        h = np.zeros(W, bool); h[rng.permutation(np.arange(1, W - 1))[:W // 2 - 1]] = True; h[W - 1] = True
        for i, j in (((15, 0), (1, 14), (8, 3)) if g % 2 == 1 else ((15, 0),)): join(ro[g], z + i, j)
        couple(rng, ro[g], z + np.flatnonzero(ro[g, z:] < 0)); couple(rng, ro[g], np.flatnonzero(ro[g, :16] < 0))
        voted(rng, ro[g], h, par[g], False)
        flip = np.zeros((W, 16), bool); np.put_along_axis(flip, rng.integers(0, 16, (W, 2)), True, 1)
        flip &= rng.random((W, 1)) < 0.75; flip[0] = False; flip[W - 1] = False
        X[g] = np.where(h[:, None] ^ flip, 255, 0)
    return pack(ro, X)
def setup_inputs_crowd(rng):
    ro = np.full((8, E), -1, np.int64); par = parities(rng, rng.permutation(N) & 3); X = np.zeros((8, W, 16), np.int64)
    for g in range(8):
        h = rng.permutation(W) < W // 2
        voted(rng, ro[g], h, par[g], g % 4 == 0)
        X[g] = rng.integers(0, 64, (W, 16)) + 192 * h[:, None]
    return pack(ro, X)
def setup_inputs_corners(rng):
    ro = np.full((8, E), -1, np.int64); a = np.arange(E); w = np.arange(W); kind = rng.permutation(8)
    for g in range(8):
        c = int(kind[g]); s = int(rng.integers(1, 16))
        if c == 0: ro[g] = a
        elif c == 1: ro[g] = a ^ s
        elif c == 2: ro[g] = E - 1 - a
        elif c == 3:
            for r in range(N): couple(rng, ro[g], 16 * V * r + np.arange(16 * V))
        elif c == 4: ro[g] = ((a + E // 2) % E) ^ s
        elif c == 5:
            step = (1, 2, 3, V, V - 1, W // 2, W - 1, 0)
            for b in range(8): join(ro[g], 16 * w + 2 * b, 16 * ((w + step[b]) % W) + 2 * b + 1)
        elif c == 6:
            q = rng.permutation(E)[:E // 2]; ro[g, q] = q; rest(rng, ro[g])
        else:
            join(ro[g], np.arange(16), E - 1 - np.arange(16)); rest(rng, ro[g])
    X = rng.integers(0, 256, (8, W, 16)); at = np.argsort(kind); o = at[rng.permutation(np.array([0, 1, 2, 4, 5]))]
    X[at[6]] = rng.integers(0, 256, 16)
    X[at[3]] = rng.integers(0, 255, 16) + rng.integers(0, 2, (W, 1))
    X[at[7]] = 255 * rng.integers(0, 2, (W, 1))
    X[o[0]] = 0; X[o[0], W - 1] = 255
    X[o[1]] = rng.integers(0, 2, (W, 16)); X[o[2]] = 255 - rng.integers(0, 3, (W, 16))
    return pack(ro, X)
def setup_inputs_ties(rng):
    ro = np.full((8, E), -1, np.int64); X = np.zeros((8, W, 16), np.int64)
    for g in range(8):
        b = rng.integers(64, 192, 16); d = rng.integers(1, 61, 16)
        X[g] = np.stack([b, b + d, b - d, b + rng.permutation(d)])[rng.integers(0, 4, W)]
        nearly(rng, ro[g], X[g])
        rest(rng, ro[g])
    return pack(ro, X)
def check_inputs(d):
    bad = []
    xf = np.asarray(d["x"]).astype(np.float64); r = np.asarray(d["rot"]).astype(np.int64)
    if not (np.min(xf) >= 0 and np.max(xf) <= 255): bad.append("range of x")
    if not np.array_equal(xf, np.floor(xf)): bad.append("whole numbers of x")
    if np.min(r) < 0 or np.max(r) > E - 1: bad.append("range of rot")
    full = np.clip(np.concatenate([gentries(a) for a in r], axis=1), 0, E - 1)
    if not np.array_equal(np.take_along_axis(full, full, 1), np.tile(np.arange(E), (8, 1))): bad.append("rot is its own inverse")
    return bad
def reference(rot, x):
    R = np.concatenate([gentries(a) for a in rot], axis=1).astype(np.int64)
    X = np.ascontiguousarray(x.astype(np.float32).astype(np.int32).reshape(N, 8, 16, V).transpose(1, 0, 3, 2)).reshape(8, W, 16)
    g = np.arange(8)[:, None]
    for t in range(RO):
        far = R >> 4
        Y = X[g, far].reshape(8, W, 16, 16)
        score = np.add.reduce(np.abs(Y - X[:, :, None, :]), axis=3)
        k = np.argmax(score, axis=2)
        A = np.add.reduce((k & 1).reshape(8, N, V), axis=(0, 2))
        m = (k + np.repeat(A, V)[None, :]) & 15; m = np.where(m == 0, 15, m)
        S = np.take_along_axis(R, 16 * far + ((R & 15) ^ m[g, far]), 1)
        X = ((2 ** SH - 1) * X + np.take_along_axis(Y, k[:, :, None, None], 2)[:, :, 0]) >> SH
        R = S
    yr = R.reshape(8, N, V, 16).transpose(1, 0, 3, 2).reshape(N, 128, V)
    yx = X.reshape(8, N, V, 16).transpose(1, 0, 3, 2).reshape(N, 128, V)
    return {"yr": np.ascontiguousarray(yr).astype(np.float32), "yx": np.ascontiguousarray(yx).astype(np.float32).astype(BF)}

@@ -1,0 +1,467 @@
+from concourse.bass import DstId, RemoteDMATransfer
+from concourse.mybir import AluOpType as Op, AxisListType, ActivationFunctionType as Fn
+
+NR, V, NP, PV = 8, 384, 6, 64
+PW = 16 * PV
+PLAN = {"x0": (7, 0), "t1": (4, 1), "x1": (7, 0), "t2": (4, 1), "x2": (7, 0), "t3": (4, 1)}
+
+BF, F32, I32, U16 = "bfloat16", "float32", "int32", "uint16"
+SCRATCH = {}
+for _n, _w, _d in [
+    ("x0", 3072, BF), ("x1", 3072, BF), ("x2", 3072, BF), ("t1", 6144, BF), ("t2", 6144, BF), ("t3", 6144, BF),
+    ("gb", 6144, BF), ("dd", 6144, BF), ("mk", 6144, BF), ("xr", 6144, BF), ("ww", 6144, BF),
+    ("xo", 384, BF), ("xq", 384, BF), ("hi", 384, BF), ("lo", 384, BF), ("rin", 384, I32), ("rs", 384, F32),
+    ("ri", 384, I32), ("rj", 384, I32), ("rk", 384, I32), ("dq", 384, I32), ("sc", 384, F32), ("d0", 384, F32),
+    ("far", 384, U16), ("of3", 384, U16), ("jl", 384, U16),
+    ("pid", 8, I32), ("pi", 8, I32), ("pf", 8, F32), ("pc", 8, F32), ("ci", 144, F32),
+    ("vq0", 24, I32), ("qb0", 24, I32), ("qw0", 24, I32), ("qw", 24, F32), ("vq", 24, U16), ("qv", 24, U16), ("qb", 24, F32), ("c16", 24, F32),
+    ("ki", 24, I32), ("par", 24, I32), ("parf", 24, BF), ("kk", 24, I32), ("ox", 24, F32), ("oxu", 24, U16),
+    ("ss", 8, F32), ("tt", 24, I32), ("yy", 24, I32), ("a0", 24, F32), ("ee", 24, F32), ("o0", 24, F32), ("o1", 24, F32),
+    ("u0", 24, U16), ("u1", 24, U16),
+    ("ones", 128, BF), ("zs", 144, BF), ("zr", 144, BF), ("z2", 144, BF), ("z3", 144, BF), ("z40", 144, BF), ("z41", 144, BF),
+    ("em", 16, BF), ("pm", 896, BF),
+]:
+    SCRATCH[_n] = ("sbuf", [128, _w], _d)
+PS = ["rna", "rnb", "r2a", "r2b", "wa", "wb", "sca", "scb"]
+for _n in PS:
+    SCRATCH[_n] = ("psum", [128, 512], F32)
+SEMAPHORES = ["sv", "sa", "sp", "sg", "ldx", "ldr", "st", "sent"] + ["ar_" + k for k in PLAN]
+
+
+def R(name, lo, hi, step=1):
+    return (name, lo, hi, step)
+
+
+def clash(a, b):
+    if a[0] != b[0] or a[1] >= b[2] or b[1] >= a[2]:
+        return False
+    return not (a[3] > 1 and a[3] == b[3] and (a[1] - b[1]) % a[3] != 0)
+
+
+def peers_of(T, rank):
+    return [T.cores[(rank + d) % NR] for d in range(1, NR)]
+
+
+def helpers_of(topo, c):
+    return [h for h in topo.cores_of(c) if topo.die(h) != topo.die(c)]
+
+
+def bits(m):
+    return bin(m).count("1")
+
+
+def dst_id(topo, d, s):
+    rid, pid = topo.addr(d, s)
+    return DstId(rid=rid, pnc=pid)
+
+
+def helper_program(g, core, T, topo):
+    own = [c for c in topo.cores_of(core) if T.rank_of(c) is not None]
+    if not own:
+        return
+    rc = own[0]
+    rank = T.rank_of(rc)
+    hs = helpers_of(topo, rc)
+    if core not in hs:
+        return
+    hi = hs.index(core)
+    peers = peers_of(T, rank)
+    on = bits(topo.mask(rc, core) & ~topo.mask(rc, peers[0]))
+    sent = 0
+    for key, (nd, nh) in PLAN.items():
+        if hi >= nh:
+            continue
+        w = T[key].shape[1] // NR
+        a, b = rank * w + hi * (w // nh), rank * w + (hi + 1) * (w // nh)
+        g.wait_ge(T.sem["ar_" + key], on // nh)
+        m = topo.mask(core, peers[nd])
+        g.remote_dma_fused([RemoteDMATransfer(dst_ids=[dst_id(topo, d, core) for d in peers[nd:]], dma_engine_mask=m,
+                                              remote_sem=T.sem["ar_" + key], srcs=[T[key][:, a:b]],
+                                              dsts=[T[key][:, a:b] for d in peers[nd:]])], local_sem=T.sem.sent)
+        sent += bits(m)
+    if sent:
+        g.wait_ge(T.sem.sent, sent)
+
+
+def rank_program(g, core, T, topo):
+    rank = T.rank_of(core)
+    if rank is None:
+        helper_program(g, core, T, topo)
+        return
+    Q = {"v": g.vector, "a": g.scalar, "p": g.tensor, "g": g, "s": g.sync}
+    SEM = {"v": "sv", "a": "sa", "p": "sp", "g": "sg"}
+    count = {}
+    known = {e: {} for e in Q}
+    clock = {}
+    log = []
+
+    def ap(r):
+        return T[r[0]][:, r[1]:r[2]] if r[3] == 1 else T[r[0]][:, r[1]:r[2]:r[3]]
+
+    def ind(win, off):
+        return ap(win).indirect(ap(off))
+
+    def wait(e, tok):
+        if known[e].get(tok[0], 0) >= tok[1]:
+            return
+        Q[e].wait_ge(T.sem[tok[0]], tok[1])
+        for s, n in clock[tok].items():
+            known[e][s] = max(known[e].get(s, 0), n)
+
+    def deps(e, reads, writes):
+        need = {}
+        for reg, w, oe, tok in log:
+            if oe == e and e == "p":
+                continue
+            hit = False
+            if reg[0] in PS and oe != e:
+                hit = any(r[0] == reg[0] for r in reads + writes)
+            else:
+                hit = any(clash(reg, r) for r in writes) or (w and any(clash(reg, r) for r in reads))
+            if hit:
+                need[tok[0]] = max(need.get(tok[0], 0), tok[1])
+        toks = sorted(need.items(), key=lambda t: -len(clock[t]))
+        for t in toks:
+            wait(e, t)
+
+    def note(e, tok, reads, writes, ck):
+        clock[tok] = dict(ck)
+        clock[tok][tok[0]] = tok[1]
+        for r in reads:
+            log.append((r, False, e, tok))
+        for r in writes:
+            log.append((r, True, e, tok))
+
+    def op(e, fn, reads, writes, sem=None):
+        deps(e, reads, writes)
+        s, n = (SEM[e], 1) if sem is None else (sem, 16)
+        fn().then_inc(T.sem[s], n)
+        count[s] = count.get(s, 0) + n
+        note(e if sem is None else "dma", (s, count[s]), reads, writes, known[e])
+
+    V_, A_ = g.vector, g.scalar
+
+    def copy(o, i, e="v"):
+        if e == "v":
+            op(e, lambda: V_.tensor_copy(ap(o), ap(i)), [i], [o])
+        else:
+            op(e, lambda: A_.activation(ap(o), ap(i), Fn.Copy), [i], [o])
+
+    def gather(o, win, off, e="v"):
+        if e == "v":
+            op(e, lambda: V_.tensor_copy(ap(o), ind(win, off)), [win, off], [o])
+        else:
+            op(e, lambda: A_.activation(ap(o), ind(win, off), Fn.Copy), [win, off], [o])
+
+    def ts(o, i, s1, op0, s2=None, op1=None, off=None):
+        rd = [i] + [s for s in (s1, s2, off) if isinstance(s, tuple)]
+        a1 = ap(s1) if isinstance(s1, tuple) else s1
+        a2 = ap(s2) if isinstance(s2, tuple) else s2
+        src = ap(i) if off is None else ind(i, off)
+        if op1 is None:
+            op("v", lambda: V_.tensor_scalar(ap(o), src, a1, None, op0), rd, [o])
+        else:
+            op("v", lambda: V_.tensor_scalar(ap(o), src, a1, a2, op0, op1), rd, [o])
+
+    def tt(o, i0, i1, alu, off=None):
+        src = ap(i0) if off is None else ind(i0, off)
+        op("v", lambda: V_.tensor_tensor(ap(o), src, ap(i1), alu), [i0, i1] + ([off] if off else []), [o])
+
+    def fill(o, c):
+        op("v", lambda: V_.memset(ap(o), c), [], [o])
+
+    def mm(o, pairs, first=True, last=True):
+        def fn():
+            for n, (l, r) in enumerate(pairs):
+                ins = g.tensor.matmul(ap(o), ap(l), ap(r), first and n == 0, last and n == len(pairs) - 1)
+            return ins
+        op("p", fn, [x for pr in pairs for x in pr], [o])
+
+    peers = peers_of(T, rank)
+    hs = helpers_of(topo, core)
+    off_mask = topo.mask(core, peers[0])
+    on_eng = [e for e in topo.engines(core, hs[0]) if e not in topo.engines(core, peers[0])]
+    sent = [0]
+
+    def own(key):
+        w = T[key].shape[1] // NR
+        return R(key, rank * w, (rank + 1) * w)
+
+    def send(key):
+        nd, nh = PLAN[key]
+        o = own(key)
+        deps("g", [o], [])
+        sem = T.sem["ar_" + key]
+        direct = RemoteDMATransfer(dst_ids=[dst_id(topo, d, core) for d in peers[:nd]], dma_engine_mask=off_mask,
+                                   remote_sem=sem, srcs=[ap(o)], dsts=[ap(o) for d in peers[:nd]])
+        hop = []
+        for h in range(nh):
+            w, ne = (o[2] - o[1]) // nh, len(on_eng) // nh
+            part = ap(R(key, o[1] + h * w, o[1] + (h + 1) * w))
+            hop.append(RemoteDMATransfer(dst_ids=[dst_id(topo, hs[h], core)],
+                                         dma_engine_mask=sum(1 << e for e in on_eng[h * ne:(h + 1) * ne]),
+                                         remote_sem=sem, srcs=[part], dsts=[part]))
+        if nh <= 1:
+            g.remote_dma_fused(hop + [direct], local_sem=T.sem.sent)
+        else:
+            g.remote_dma_fused(hop, local_sem=T.sem.sent)
+            g.remote_dma_fused([direct], local_sem=T.sem.sent)
+        sent[0] += bits(off_mask) + (len(on_eng) if nh else 0)
+        total = bits(off_mask) * (nd + (NR - 1 - nd) * nh)
+        note("dma", ("ar_" + key, total), [], [R(key, 0, o[1]), R(key, o[2], T[key].shape[1])], {})
+
+    def iota(o, pat, base, cm):
+        if SCRATCH[o[0]][2] == I32:
+            op("g", lambda: g.iota(ap(o), pat, base, cm), [], [o])
+        else:
+            op("g", lambda: g.iota(ap(o), pat, base, cm, allow_small_or_imprecise_dtypes=True), [], [o])
+
+    def perm(m):
+        pats = {1: [[2, 64], [-1, 2]], 2: [[4, 32], [-2, 2], [1, 2]], 3: [[4, 32], [-1, 4]], 4: [[8, 16], [-4, 2], [1, 4]],
+                6: [[8, 16], [-2, 4], [1, 2]], 7: [[8, 16], [-1, 8]]}
+        c0 = 128 * (m - 1)
+        if m in pats:
+            parts = [(R("pm", c0, c0 + 128), R("ones", 0, 128), pats[m], m)]
+        else:
+            parts = [(R("pm", c0 + b, c0 + 128, 2), R("ones", 0, 64), [[8, 16], [-4, 2], [2, 2]], m - b) for b in (0, 1)]
+        for o, i, pat, base in parts:
+            op("g", lambda: g.affine_select(ap(o), ap(i), pat, Op.is_equal, 0.0, base, -1), [i], [o])
+
+    full = lambda n: R(n, 0, SCRATCH[n][1][1])
+    col = lambda n, c: R(n, c, c + 1)
+
+    def wat(part, b0, b1):
+        return R("ww", 2048 * part + 128 * b0, 2048 * part + 128 * b1)
+
+    WG = ((1, 5), (5, 8), (9, 13), (13, 16))
+
+    def w_mm(part, n):
+        for b in range(*WG[n]):
+            m, c = 16 - b, 128 * (b - WG[n][0])
+            src = (16 - (m & 8)) & 15
+            mm(R(("wa", "wb")[n % 2], c, c + 128), [(R("pm", 128 * ((m & 7) - 1), 128 * (m & 7)), wat(part, src, src + 1))])
+
+    def w_copy(part, n, e="a"):
+        b0, b1 = WG[n]
+        copy(wat(part, b0, b1), R(("wa", "wb")[n % 2], 0, 128 * (b1 - b0)), e)
+
+    def w_half(part, h):
+        return [lambda: w_mm(part, 2 * h), lambda: w_mm(part, 2 * h + 1), lambda: w_copy(part, 2 * h), lambda: w_copy(part, 2 * h + 1)]
+
+    def t_gather(key, p):
+        tt(R("gb", p * PW, (p + 1) * PW), full(key), R("mk", p * PW, (p + 1) * PW), Op.mult, off=R("of3", p * PV, (p + 1) * PV))
+
+    def rn_bank(p):
+        return R(("rna", "rnb")[p % 2], 0, PV)
+
+    def rn(p):
+        mm(rn_bank(p), [(R("zr", 15 - i, 143 - i), R("gb", p * PW + i, (p + 1) * PW, 16)) for i in range(16)])
+
+    def r2(p):
+        name, c = ("r2a", "r2b")[p // 2 % 2], p % 2 * PV
+        for ih in (0, 1):
+            mm(R(name, ih * 128 + c, ih * 128 + c + PV),
+               [(R("z2", 7 - i, 135 - i), R("gb", p * PW + 8 * ih + i, (p + 1) * PW, 16)) for i in range(8)])
+
+    def r2copy(part):
+        for ih in (0, 1):
+            copy(wat(part, 8 * ih, 8 * ih + 1), R(("r2a", "r2b")[part % 2], ih * 128, (ih + 1) * 128), "a")
+
+    def rn2(part):
+        mm(R(("rna", "rnb")[part % 2], 0, 128), [(R("z3", 8 - 8 * ih, 136 - 8 * ih), wat(part, 8 * ih, 8 * ih + 1)) for ih in (0, 1)])
+
+    def far(part):
+        src = R(("rna", "rnb")[part % 2], 0, 128)
+        ts(R("far", part * 128, (part + 1) * 128), src, -7.5, Op.add, 0.0625, Op.mult)
+        copy(R("rs", part * 128, (part + 1) * 128), src, "a")
+
+    def rs(p):
+        copy(R("rs", p * PV, (p + 1) * PV), rn_bank(p), "a")
+
+    def x_gather(key, c0, c1):
+        tt(R("dd", 16 * c0, 16 * c1), full(key), R("xr", 16 * c0, 16 * c1), Op.subtract, off=R("far", c0, c1))
+
+    def absd(c0, c1):
+        o, i = R("gb", 16 * c0, 16 * c1), R("dd", 16 * c0, 16 * c1)
+        op("a", lambda: A_.activation(ap(o), ap(i), Fn.Abs), [i], [o])
+
+    def score(p, s0=0, s1=16):
+        o = R("sca", p * PV, (p + 1) * PV) if p < NP - 1 else R("scb", 0, PV)
+        mm(o, [(R("zs", 15 - s, 143 - s), R("gb", p * PW + 64 * s, p * PW + 64 * (s + 1))) for s in range(s0, s1)],
+           s0 == 0, s1 == 16)
+
+    def scan(c0, c1, src):
+        o, d = R("sc", c0, c1), R("d0", c0, c1)
+        op("v", lambda: V_.tensor_tensor_scan(ap(o), ap(d), ap(src), 0.0, Op.add, Op.max), [d, src], [o])
+
+    def lists():
+        ts(full("rj"), full("ri"), 7, Op.bitwise_and)
+        ts(full("of3"), full("ri"), -3.5, Op.add, 0.125, Op.mult)
+        copy(full("jl"), full("rj"))
+
+    def mask(p):
+        gather(R("mk", p * PW, (p + 1) * PW), full("em"), R("jl", p * PV, (p + 1) * PV), "a")
+
+    def xrep(key, on_a=0):
+        gather(full("xq"), own(key), full("vq"))
+        for i in range(on_a):
+            copy(R("xr", i, 6144, 16), full("xq"), "a")
+        return [lambda i=i: copy(R("xr", i, 6144, 16), full("xq")) for i in range(on_a, 16)]
+
+    def x_phase(t, extra):
+        key = "x%d" % (t - 1)
+        for p in range(NP):
+            if p < NP - 1:
+                x_gather(key, p * PV, (p + 1) * PV)
+            else:
+                x_gather(key, p * PV, p * PV + 32)
+                x_gather(key, p * PV + 32, p * PV + 48)
+                x_gather(key, p * PV + 48, p * PV + 64)
+            for f in extra[p][0]:
+                f()
+            if p >= 1:
+                absd((p - 1) * PV, p * PV)
+                score(p - 1)
+            for f in extra[p][1]:
+                f()
+        c = (NP - 1) * PV
+        absd(c, c + 32)
+        score(NP - 1, 0, 8)
+        absd(c + 32, c + 48)
+        score(NP - 1, 8, 12)
+        absd(c + 48, c + 64)
+        score(NP - 1, 12, 16)
+        scan(0, c, R("sca", 0, c))
+        if t == 3:
+            gather(full("ri"), full("rs"), full("qv"))
+        elif t == 2:
+            copy(full("ri"), full("rs"))
+        scan(c, V, R("scb", 0, PV))
+
+    def tail(t):
+        tk = "t%d" % t
+        keys = R("sc", 15, V, 16)
+        copy(full("ki"), keys)
+        ts(full("par"), full("ki"), 1, Op.bitwise_and)
+        copy(full("parf"), full("par"))
+        mm(R("sca", 0, 24), [(full("ones"), full("parf"))])
+        ts(full("kk"), full("ki"), 15, Op.bitwise_and)
+        op("v", lambda: V_.tensor_reduce(ap(col("ss", 0)), ap(R("sca", 0, 24)), AxisListType.X, Op.add),
+           [R("sca", 0, 24)], [col("ss", 0)])
+        ts(full("tt"), keys, col("ss", 0), Op.add, 1.0, Op.add)
+        ts(full("yy"), full("tt"), 15, Op.bitwise_and)
+        ts(full("a0"), full("yy"), 1.0, Op.max, 128.0, Op.mult)
+        ts(full("ee"), full("yy"), 8.0, Op.is_lt, 2048.0, Op.mult)
+        tt(full("o0"), full("a0"), full("qw"), Op.add)
+        copy(full("u0"), full("o0"))
+        tt(full("o1"), full("o0"), full("ee"), Op.add)
+        o = own(tk)
+        gather(R(tk, o[1], o[2], 2), full("ww"), full("u0"), "a")
+        ts(full("u1"), full("o1"), -1024.0, Op.add)
+        gather(R(tk, o[1] + 1, o[2], 2), full("ww"), full("u1"))
+        send(tk)
+        if t > 1:
+            lists()
+        tt(full("ox"), full("c16"), full("kk"), Op.subtract)
+        copy(full("oxu"), full("ox"))
+        ts(full("dq"), full("dd"), -1.5, Op.add, 0.25, Op.mult, off=full("oxu"))
+        nxt = own("x%d" % t) if t < 3 else full("xo")
+        tt(nxt, full("dq"), own("x%d" % (t - 1)), Op.add)
+        if t < 3:
+            send("x%d" % t)
+        else:
+            op("s", lambda: g.sync.dma_start(T.yx[:], ap(nxt)), [nxt], [], sem="st")
+        for p in range(NP):
+            mask(p)
+        if t < 3:
+            for f in xrep("x%d" % t):
+                f()
+
+    op("s", lambda: g.sync.dma_start(ap(own("x0")), T.x[:]), [], [own("x0")], sem="ldx")
+    op("a", lambda: g.scalar.dma_start(ap(full("rin")), T.rot[:]), [], [full("rin")], sem="ldr")
+    iota(col("pid", 0), [[0, 1]], 0, 1)
+    iota(full("vq0"), [[64, 6], [4, 4]], 0, 0)
+    iota(full("ci"), [[1, 144]], -15, 0)
+    iota(full("qb0"), [[64, 6], [1, 4]], 0, 0)
+    fill(full("ones"), 1.0)
+    fill(full("d0"), 1.0)
+    perm(1)
+    perm(2)
+    send("x0")
+    for m in range(3, 8):
+        perm(m)
+    iota(full("qw0"), [[2048, 3], [64, 2], [1, 4]], 0, 0)
+    for c, mk in enumerate((0x70, 0x78, 0x77, 7, 8, 3, None, 15)):
+        if mk is None:
+            ts(col("pi", c), col("pid", 0), 2, Op.logical_shift_right, 3, Op.bitwise_and)
+        else:
+            ts(col("pi", c), col("pid", 0), mk, Op.bitwise_and)
+    fill(R("d0", 0, V, 16), -1.0e6)
+    copy(full("pf"), full("pi"))
+    ts(col("pc", 0), col("pf", 5), 16.0, Op.mult, col("pf", 6), Op.add)
+    ts(col("pc", 1), col("pf", 4), 0.125, Op.mult)
+    ts(col("pc", 2), col("pf", 4), -0.125, Op.mult, 1.0, Op.add)
+    ts(full("vq"), full("vq0"), col("pc", 0), Op.add)
+    ts(R("z40", 0, 136), R("ci", 7, 143), col("pf", 2), Op.is_equal, col("pc", 2), Op.mult)
+    ts(R("z41", 0, 136), R("ci", 7, 143), col("pf", 2), Op.is_equal, col("pc", 1), Op.mult)
+    rest = xrep("x0", 5)
+    gather(full("ri"), full("rin"), full("vq"))
+    ts(full("rj"), full("ri"), 8, Op.logical_shift_right)
+    ts(full("rk"), full("ri"), 255, Op.bitwise_and)
+    copy(full("hi"), full("rj"))
+    copy(full("lo"), full("rk"))
+    for ih, name in ((0, "r2a"), (1, "r2b")):
+        z = "z4%d" % ih
+        mm(R(name, 0, V), [(R(z, 8, 136), full("hi")), (R(z, 0, 128), full("lo"))])
+        for part in range(3):
+            copy(wat(part, 8 * ih, 8 * ih + 1), R(name, 128 * part, 128 * (part + 1)), "a")
+    ts(full("far"), full("ri"), -7.5, Op.add, 0.0625, Op.mult)
+    for f in rest:
+        f()
+    for part in range(3):
+        for f in w_half(part, 0) + w_half(part, 1):
+            f()
+    ts(R("zs", 0, 143), R("ci", 0, 143), col("pf", 0), Op.is_equal, 16.0, Op.mult)
+    ts(col("pc", 3), col("pf", 7), 4.0, Op.mult)
+    ts(col("pc", 4), col("pf", 4), -31.875, Op.mult, 256.0, Op.add)
+    ts(full("em"), R("ci", 15, 31), col("pf", 3), Op.is_equal)
+    ts(full("qb"), full("qb0"), col("pc", 3), Op.add)
+    ts(full("qw"), full("qw0"), col("pc", 3), Op.add)
+    ts(full("c16"), full("qb"), 16.0, Op.mult, 15.0, Op.add)
+    copy(full("qv"), full("qb"))
+    lists()
+
+    x_phase(1, [([], [])] * NP)
+    tail(1)
+    ts(R("zr", 0, 143), R("ci", 0, 143), col("pf", 0), Op.is_equal, col("pc", 4), Op.mult)
+    ts(R("z3", 0, 136), R("ci", 7, 143), col("pf", 2), Op.is_equal, col("pc", 4), Op.mult)
+    ts(R("z2", 0, 135), R("ci", 8, 143), col("pf", 1), Op.is_equal)
+
+    for t in (2, 3):
+        tk = "t%d" % (t - 1)
+        for p in range(NP):
+            t_gather(tk, p)
+            if p >= 2:
+                for f in w_half(p // 2 - 1, p % 2):
+                    f()
+            if p in (3, 5):
+                far(p // 2 - 1)
+            r2(p)
+            if p % 2:
+                r2copy(p // 2)
+                rn2(p // 2)
+        x_phase(t, [(w_half(2, 0), []), (w_half(2, 1) + [lambda: far(2)], [])] + [([], [])] * 4)
+        tail(t)
+
+    cuts = {2: 0, 4: 3 * PV, 5: 5 * PV}
+    for p in range(NP):
+        t_gather("t3", p)
+        rn(p)
+        rs(p)
+        if p in cuts:
+            a, b = cuts[p], (p + 1) * PV
+            op("s", lambda: g.sync.dma_start(T.yr[:, a:b], ap(R("rs", a, b))), [R("rs", a, b)], [], sem="st")
+    g.sync.wait_ge(T.sem.st, count["st"])
+    g.wait_ge(T.sem.sent, sent[0])
+    for s in ("sv", "sa", "sp", "sg"):
+        g.wait_ge(T.sem[s], count[s])

@@ -3,7 +3,37 @@ from concourse.mybir import AluOpType as Op, AxisListType, ActivationFunctionTyp
 
 NR, V, NP, PV = 8, 384, 6, 64
 PW = 16 * PV
-PLAN = {"x0": (7, 0), "t1": (4, 1), "x1": (7, 0), "t2": (4, 1), "x2": (7, 0), "t3": (4, 1)}
+CH = PW // 2
+ND = {1: 1, 2: 1, 3: 1}
+ABS = {t: range(NP) for t in (1, 2, 3)}
+TS = {1: (2, 3), 2: (2, 3), 3: (3, 6, 7)}
+WENG = "aaxxxx"
+MENG = {1: "xxxxxx", 2: "xxxxxx", 3: "xxxxxx"}
+SU = 2
+WLATE = 9
+TBK = ("wa", "wb", "da", "db", "sca")
+FAR0 = 0
+XG = 12
+XG0 = 8
+FU = 3
+WB = ("da", "db", "wa", "wb")
+STAT = (0, 1, 2)
+STAT3 = (0, 1)
+XORD = {1: (0, 1, 2, 3, 4, 5), 2: (0, 1, 2, 3, 4, 5), 3: (0, 1, 2, 3, 4, 5)}
+WU = 0
+TCUT = 2
+T_LANES = ((None, 0, 2, 0, 4), (1, 0, 2, 4, 7), (2, 1, 2, 4, 7), (0, 1, 2, 1, 4), (None, 1, 2, 0, 1))
+X_LANES = ((1, 0, 1, 0, 2), (2, 0, 1, 2, 4), (0, 0, 1, 4, 7))
+X0_LANES = ((None, 0, 1, 0, 4), (1, 0, 1, 4, 5), (2, 0, 1, 5, 6), (0, 0, 1, 6, 7))
+PLAN = {"x0": X0_LANES, "t1": T_LANES, "x1": X_LANES, "t2": T_LANES, "x2": X_LANES, "t3": T_LANES}
+FIX, LOCAL = 60, 2600
+WAKE = 140
+SLACK = 100
+FUSED = 1.56
+AFIX = 60
+GATHER = 1.56
+COLUMN = 1.0
+EXCHANGE = {"x0": 10000, "t1": 8000, "x1": 9500, "t2": 8000, "x2": 9500, "t3": 8000}
 
 BF, F32, I32, U16 = "bfloat16", "float32", "int32", "uint16"
 SCRATCH = {}
@@ -12,20 +42,22 @@ for _n, _w, _d in [
     ("gb", 6144, BF), ("dd", 6144, BF), ("mk", 6144, BF), ("xr", 6144, BF), ("ww", 6144, BF),
     ("xo", 384, BF), ("xq", 384, BF), ("hi", 384, BF), ("lo", 384, BF), ("rin", 384, I32), ("rs", 384, F32),
     ("ri", 384, I32), ("rj", 384, I32), ("rk", 384, I32), ("dq", 384, I32), ("sc", 384, F32), ("d0", 384, F32),
-    ("far", 384, U16), ("of3", 384, U16), ("jl", 384, U16),
+    ("zz", 384, F32), ("far", 384, U16), ("of3", 384, U16), ("jl", 384, U16),
     ("pid", 8, I32), ("pi", 8, I32), ("pf", 8, F32), ("pc", 8, F32), ("ci", 144, F32),
     ("vq0", 24, I32), ("qb0", 24, I32), ("qw0", 24, I32), ("qw", 24, F32), ("vq", 24, U16), ("qv", 24, U16), ("qb", 24, F32), ("c16", 24, F32),
     ("ki", 24, I32), ("par", 24, I32), ("parf", 24, BF), ("kk", 24, I32), ("ox", 24, F32), ("oxu", 24, U16),
     ("ss", 8, F32), ("tt", 24, I32), ("yy", 24, I32), ("a0", 24, F32), ("ee", 24, F32), ("o0", 24, F32), ("o1", 24, F32),
     ("u0", 24, U16), ("u1", 24, U16),
-    ("ones", 128, BF), ("zs", 144, BF), ("zr", 144, BF), ("z2", 144, BF), ("z3", 144, BF), ("z40", 144, BF), ("z41", 144, BF),
-    ("em", 16, BF), ("pm", 896, BF),
+    ("ones", 128, BF), ("zs", 144, BF), ("zp", 144, BF), ("zn", 144, BF), ("zr", 144, BF), ("z2", 144, BF), ("z3", 144, BF),
+    ("z40", 144, BF), ("z41", 144, BF), ("e1", 128, BF), ("e4", 128, BF), ("e0", 128, BF), ("en", 128, BF), ("e256", 128, BF),
+    ("em", 256, BF), ("em0", 256, BF), ("z5", 144, BF), ("z6", 16, BF), ("z7", 16, BF), ("aa", 512, BF), ("pj", 8, I32), ("pm", 896, BF),
 ]:
     SCRATCH[_n] = ("sbuf", [128, _w], _d)
-PS = ["rna", "rnb", "r2a", "r2b", "wa", "wb", "sca", "scb"]
+PS = ["ra", "rb", "da", "db", "wa", "wb", "sca", "scb"]
 for _n in PS:
     SCRATCH[_n] = ("psum", [128, 512], F32)
 SEMAPHORES = ["sv", "sa", "sp", "sg", "ldx", "ldr", "st", "sent"] + ["ar_" + k for k in PLAN]
+ORDER = []
 
 
 def R(name, lo, hi, step=1):
@@ -43,7 +75,9 @@ def peers_of(T, rank):
 
 
 def helpers_of(topo, c):
-    return [h for h in topo.cores_of(c) if topo.die(h) != topo.die(c)]
+    near = [h for h in topo.cores_of(c) if h != c and topo.die(h) == topo.die(c)]
+    far = [h for h in topo.cores_of(c) if topo.die(h) != topo.die(c)]
+    return [near[0], far[0], far[1]]
 
 
 def bits(m):
@@ -55,6 +89,15 @@ def dst_id(topo, d, s):
     return DstId(rid=rid, pnc=pid)
 
 
+def part_of(T, key, rank, part, parts):
+    w = T[key].shape[1] // NR
+    return rank * w + part * w // parts, rank * w + (part + 1) * w // parts
+
+
+def hop_mask(topo, rc, peer, helper):
+    return topo.mask(rc, helper) & ~topo.mask(rc, peer)
+
+
 def helper_program(g, core, T, topo):
     own = [c for c in topo.cores_of(core) if T.rank_of(c) is not None]
     if not own:
@@ -64,21 +107,19 @@ def helper_program(g, core, T, topo):
     hs = helpers_of(topo, rc)
     if core not in hs:
         return
-    hi = hs.index(core)
     peers = peers_of(T, rank)
-    on = bits(topo.mask(rc, core) & ~topo.mask(rc, peers[0]))
     sent = 0
-    for key, (nd, nh) in PLAN.items():
-        if hi >= nh:
-            continue
-        w = T[key].shape[1] // NR
-        a, b = rank * w + hi * (w // nh), rank * w + (hi + 1) * (w // nh)
-        g.wait_ge(T.sem["ar_" + key], on // nh)
-        m = topo.mask(core, peers[nd])
-        g.remote_dma_fused([RemoteDMATransfer(dst_ids=[dst_id(topo, d, core) for d in peers[nd:]], dma_engine_mask=m,
-                                              remote_sem=T.sem["ar_" + key], srcs=[T[key][:, a:b]],
-                                              dsts=[T[key][:, a:b] for d in peers[nd:]])], local_sem=T.sem.sent)
-        sent += bits(m)
+    for key, lanes in PLAN.items():
+        for who, part, parts, p0, p1 in lanes:
+            if who != hs.index(core):
+                continue
+            a, b = part_of(T, key, rank, part, parts)
+            g.wait_ge(T.sem["ar_" + key], bits(hop_mask(topo, rc, peers[0], core)))
+            m = topo.mask(core, peers[p0])
+            g.remote_dma_fused([RemoteDMATransfer(dst_ids=[dst_id(topo, d, core) for d in peers[p0:p1]], dma_engine_mask=m,
+                                                  remote_sem=T.sem["ar_" + key], srcs=[T[key][:, a:b]],
+                                                  dsts=[T[key][:, a:b] for d in peers[p0:p1]])], local_sem=T.sem.sent)
+            sent += bits(m)
     if sent:
         g.wait_ge(T.sem.sent, sent)
 
@@ -132,26 +173,100 @@ def rank_program(g, core, T, topo):
         for r in writes:
             log.append((r, True, e, tok))
 
-    def op(e, fn, reads, writes, sem=None):
+    tasks, other, turns, gates, urgent = [], {}, {}, {}, {}
+
+    def op(e, fn, reads, writes, cost, sem=None, late=0, landed=None):
+        tasks.append((e, fn, reads, writes, cost, sem, late, landed))
+
+    def issue(e, fn, reads, writes, cost, sem, late, landed):
+        if landed is not None:
+            deps(e, reads, [])
+            fn()
+            note("dma", landed, [], writes, {})
+            return
         deps(e, reads, writes)
         s, n = (SEM[e], 1) if sem is None else (sem, 16)
         fn().then_inc(T.sem[s], n)
         count[s] = count.get(s, 0) + n
         note(e if sem is None else "dma", (s, count[s]), reads, writes, known[e])
 
+    def order():
+        n = len(tasks)
+        before, seen = [set() for _ in range(n)], {}
+        for i, t in enumerate(tasks):
+            for regs, w in ((t[2], False), (t[3], True)):
+                for r in regs:
+                    before[i].update(j for q, qw, j in seen.get(r[0], ()) if (w or qw) and clash(q, r))
+            for regs, w in ((t[2], False), (t[3], True)):
+                for r in regs:
+                    seen.setdefault(r[0], []).append((r, w, i))
+        for row in turns.values():
+            for a, b in zip(row, row[1:]):
+                before[b].add(a)
+        after = [[] for _ in range(n)]
+        for i in range(n):
+            before[i].update(j for j in gates if j < i and tasks[i][0] in "vap" and i < gates[j])
+            for j in before[i]:
+                after[j].append(i)
+        left, ready, free, bank = [len(b) for b in before], [0.0] * n, {e: 0.0 for e in Q}, {}
+        cand, out = {i for i in range(n) if not left[i]}, []
+        banks = [{r[0] for r in t[2] + t[3] if r[0] in PS} for t in tasks]
+
+        def start(i, e):
+            return max([ready[i], free[e]] + [bank[b][1] + WAKE for b in banks[i] if b in bank and bank[b][0] != e])
+        while cand:
+            st = {(i, t[0]): (start(i, t[0]), t) for i in cand for t in [tasks[i]] + other.get(i, [])}
+            first = min(st, key=lambda k: (st[k][0], k))
+            e = first[1]
+            k = min((k for k in st if k[1] == e and st[k][0] <= st[first][0] + SLACK), key=lambda k: (-urgent.get(k[0], 0), k))
+            i, t = k[0], st[k][1]
+            cand.remove(i)
+            out.append(k)
+            free[e] = st[k][0] + t[4]
+            for b in banks[i]:
+                bank[b] = (e, free[e])
+            for j in after[i]:
+                linked = (e, tasks[j][0]) != ("p", "p") and any(clash(a, b) for a in t[2] + t[3] for b in tasks[j][2] + tasks[j][3])
+                ready[j] = max(ready[j], free[e] + (t[6] + WAKE if linked else 0))
+                left[j] -= 1
+                if not left[j]:
+                    cand.add(j)
+        return out
+
+    def in_turn(name):
+        turns.setdefault(name, []).append(len(tasks) - 1)
+
+    def either(f):
+        f("v")
+        alt = tasks.pop()
+        f("a")
+        other[len(tasks) - 1] = [alt]
+
     V_, A_ = g.vector, g.scalar
+    size = lambda r: len(range(r[1], r[2], r[3]))
+    short = lambda *rs: all(SCRATCH[r[0]][2] in (BF, U16) for r in rs)
+
+    def cycles(o, i, off=None, rate=1.0):
+        return FIX + (FUSED if rate > 1 else GATHER) * size(o) if off else max(64, rate * size(o) * (0.5 if short(o, i) else 1))
 
     def copy(o, i, e="v"):
-        if e == "v":
-            op(e, lambda: V_.tensor_copy(ap(o), ap(i)), [i], [o])
+        if e == "any":
+            either(lambda e: copy(o, i, e))
+        elif e == "v":
+            op(e, lambda: V_.tensor_copy(ap(o), ap(i)), [i], [o], cycles(o, i))
         else:
-            op(e, lambda: A_.activation(ap(o), ap(i), Fn.Copy), [i], [o])
+            act(o, i, Fn.Copy)
 
-    def gather(o, win, off, e="v"):
-        if e == "v":
-            op(e, lambda: V_.tensor_copy(ap(o), ind(win, off)), [win, off], [o])
+    def act(o, i, fn, **kw):
+        op("a", lambda: A_.activation(ap(o), ap(i), fn, **kw), [i], [o], AFIX + size(o))
+
+    def gather(o, win, off, e="v", scale=1.0):
+        if e == "any":
+            either(lambda e: gather(o, win, off, e))
+        elif e == "v":
+            op(e, lambda: V_.tensor_copy(ap(o), ind(win, off)), [win, off], [o], cycles(o, win, off))
         else:
-            op(e, lambda: A_.activation(ap(o), ind(win, off), Fn.Copy), [win, off], [o])
+            op(e, lambda: A_.activation(ap(o), ind(win, off), Fn.Copy, scale=scale), [win, off], [o], cycles(o, win, off))
 
     def ts(o, i, s1, op0, s2=None, op1=None, off=None):
         rd = [i] + [s for s in (s1, s2, off) if isinstance(s, tuple)]
@@ -159,28 +274,27 @@ def rank_program(g, core, T, topo):
         a2 = ap(s2) if isinstance(s2, tuple) else s2
         src = ap(i) if off is None else ind(i, off)
         if op1 is None:
-            op("v", lambda: V_.tensor_scalar(ap(o), src, a1, None, op0), rd, [o])
+            op("v", lambda: V_.tensor_scalar(ap(o), src, a1, None, op0), rd, [o], cycles(o, i, off))
         else:
-            op("v", lambda: V_.tensor_scalar(ap(o), src, a1, a2, op0, op1), rd, [o])
+            op("v", lambda: V_.tensor_scalar(ap(o), src, a1, a2, op0, op1), rd, [o], cycles(o, i, off))
 
     def tt(o, i0, i1, alu, off=None):
         src = ap(i0) if off is None else ind(i0, off)
-        op("v", lambda: V_.tensor_tensor(ap(o), src, ap(i1), alu), [i0, i1] + ([off] if off else []), [o])
+        op("v", lambda: V_.tensor_tensor(ap(o), src, ap(i1), alu), [i0, i1] + ([off] if off else []), [o], cycles(o, i0, off, 2))
 
     def fill(o, c):
-        op("v", lambda: V_.memset(ap(o), c), [], [o])
+        op("v", lambda: V_.memset(ap(o), c), [], [o], cycles(o, o))
 
     def mm(o, pairs, first=True, last=True):
         def fn():
             for n, (l, r) in enumerate(pairs):
                 ins = g.tensor.matmul(ap(o), ap(l), ap(r), first and n == 0, last and n == len(pairs) - 1)
             return ins
-        op("p", fn, [x for pr in pairs for x in pr], [o])
+        op("p", fn, [x for pr in pairs for x in pr], [o], COLUMN * len(pairs) * max(64, size(o)))
 
     peers = peers_of(T, rank)
     hs = helpers_of(topo, core)
     off_mask = topo.mask(core, peers[0])
-    on_eng = [e for e in topo.engines(core, hs[0]) if e not in topo.engines(core, peers[0])]
     sent = [0]
 
     def own(key):
@@ -188,33 +302,35 @@ def rank_program(g, core, T, topo):
         return R(key, rank * w, (rank + 1) * w)
 
     def send(key):
-        nd, nh = PLAN[key]
+        lanes = PLAN[key]
+        parts = lanes[0][2]
         o = own(key)
-        deps("g", [o], [])
         sem = T.sem["ar_" + key]
-        direct = RemoteDMATransfer(dst_ids=[dst_id(topo, d, core) for d in peers[:nd]], dma_engine_mask=off_mask,
-                                   remote_sem=sem, srcs=[ap(o)], dsts=[ap(o) for d in peers[:nd]])
-        hop = []
-        for h in range(nh):
-            w, ne = (o[2] - o[1]) // nh, len(on_eng) // nh
-            part = ap(R(key, o[1] + h * w, o[1] + (h + 1) * w))
-            hop.append(RemoteDMATransfer(dst_ids=[dst_id(topo, hs[h], core)],
-                                         dma_engine_mask=sum(1 << e for e in on_eng[h * ne:(h + 1) * ne]),
-                                         remote_sem=sem, srcs=[part], dsts=[part]))
-        if nh <= 1:
-            g.remote_dma_fused(hop + [direct], local_sem=T.sem.sent)
-        else:
-            g.remote_dma_fused(hop, local_sem=T.sem.sent)
-            g.remote_dma_fused([direct], local_sem=T.sem.sent)
-        sent[0] += bits(off_mask) + (len(on_eng) if nh else 0)
-        total = bits(off_mask) * (nd + (NR - 1 - nd) * nh)
-        note("dma", ("ar_" + key, total), [], [R(key, 0, o[1]), R(key, o[2], T[key].shape[1])], {})
+        total = bits(off_mask) * sum(p1 - p0 for who, pt, n, p0, p1 in lanes)
+        for part in range(parts):
+            mine = R(key, *part_of(T, key, rank, part, parts))
+            src, trs = ap(mine), []
+            to = [(hop_mask(topo, core, peers[0], hs[0]), [hs[who] for who, pt, n, p0, p1 in lanes if who is not None and pt == part])]
+            to += [(off_mask, peers[p0:p1]) for who, pt, n, p0, p1 in lanes if who is None and pt == part]
+            for m, cores in to:
+                if cores:
+                    trs.append(RemoteDMATransfer(dst_ids=[dst_id(topo, d, core) for d in cores], dma_engine_mask=m,
+                                                 remote_sem=sem, srcs=[src], dsts=[src for d in cores]))
+                    sent[0] += bits(m)
+            last = part == parts - 1
+            op("g", lambda trs=trs: g.remote_dma_fused(trs, local_sem=T.sem.sent), [mine],
+               [R(key, 0, o[1]), R(key, o[2], T[key].shape[1])] if last else [],
+               400, late=EXCHANGE[key] if last else 0, landed=("ar_" + key, total))
+            in_turn("send")
+
+    def dma(e, out, in_, reads, writes, sem):
+        op(e, lambda: Q[e].dma_start(out, in_), reads, writes, 100, sem=sem, late=LOCAL)
 
     def iota(o, pat, base, cm):
         if SCRATCH[o[0]][2] == I32:
-            op("g", lambda: g.iota(ap(o), pat, base, cm), [], [o])
+            op("g", lambda: g.iota(ap(o), pat, base, cm), [], [o], 160 + 2 * size(o))
         else:
-            op("g", lambda: g.iota(ap(o), pat, base, cm, allow_small_or_imprecise_dtypes=True), [], [o])
+            op("g", lambda: g.iota(ap(o), pat, base, cm, allow_small_or_imprecise_dtypes=True), [], [o], 160 + 2 * size(o))
 
     def perm(m):
         pats = {1: [[2, 64], [-1, 2]], 2: [[4, 32], [-2, 2], [1, 2]], 3: [[4, 32], [-1, 4]], 4: [[8, 16], [-4, 2], [1, 4]],
@@ -225,10 +341,12 @@ def rank_program(g, core, T, topo):
         else:
             parts = [(R("pm", c0 + b, c0 + 128, 2), R("ones", 0, 64), [[8, 16], [-4, 2], [2, 2]], m - b) for b in (0, 1)]
         for o, i, pat, base in parts:
-            op("g", lambda: g.affine_select(ap(o), ap(i), pat, Op.is_equal, 0.0, base, -1), [i], [o])
+            op("g", lambda o=o, i=i, pat=pat, base=base: g.affine_select(ap(o), ap(i), pat, Op.is_equal, 0.0, base, -1),
+               [i], [o], 200 + 2 * size(o))
 
     full = lambda n: R(n, 0, SCRATCH[n][1][1])
     col = lambda n, c: R(n, c, c + 1)
+    wide = lambda n, c0, c1: R(n, 16 * c0, 16 * c1)
 
     def wat(part, b0, b1):
         return R("ww", 2048 * part + 128 * b0, 2048 * part + 128 * b1)
@@ -239,115 +357,192 @@ def rank_program(g, core, T, topo):
         for b in range(*WG[n]):
             m, c = 16 - b, 128 * (b - WG[n][0])
             src = (16 - (m & 8)) & 15
-            mm(R(("wa", "wb")[n % 2], c, c + 128), [(R("pm", 128 * ((m & 7) - 1), 128 * (m & 7)), wat(part, src, src + 1))])
+            mm(R(WB[n % len(WB)], c, c + 128), [(R("pm", 128 * ((m & 7) - 1), 128 * (m & 7)), wat(part, src, src + 1))])
+            urgent[len(tasks) - 1] = WU
 
     def w_copy(part, n, e="a"):
         b0, b1 = WG[n]
-        copy(wat(part, b0, b1), R(("wa", "wb")[n % 2], 0, 128 * (b1 - b0)), e)
+        copy(wat(part, b0, b1), R(WB[n % len(WB)], 0, 128 * (b1 - b0)), e)
 
-    def w_half(part, h):
-        return [lambda: w_mm(part, 2 * h), lambda: w_mm(part, 2 * h + 1), lambda: w_copy(part, 2 * h), lambda: w_copy(part, 2 * h + 1)]
+    def w_half(part, h, e="a"):
+        w_mm(part, 2 * h)
+        w_mm(part, 2 * h + 1)
+        w_copy(part, 2 * h, e)
+        w_copy(part, 2 * h + 1, e)
 
-    def t_gather(key, p):
-        tt(R("gb", p * PW, (p + 1) * PW), full(key), R("mk", p * PW, (p + 1) * PW), Op.mult, off=R("of3", p * PV, (p + 1) * PV))
+    last_t = []
 
-    def rn_bank(p):
-        return R(("rna", "rnb")[p % 2], 0, PV)
+    def t_gather(key, c0, c1):
+        tt(wide("gb", c0, c1), full(key), wide("mk", c0, c1), Op.mult, off=R("of3", c0, c1))
+        last_t.append(len(tasks) - 1)
 
-    def rn(p):
-        mm(rn_bank(p), [(R("zr", 15 - i, 143 - i), R("gb", p * PW + i, (p + 1) * PW, 16)) for i in range(16)])
+    def chunk(p, h):
+        return p * PV + h * PV // 2, p * PV + (h + 1) * PV // 2
+
+    def s_gather(kind, key, p, h):
+        c0, c1 = chunk(p, h)
+        if kind == "t":
+            gather(wide("dd", c0, c1), full(key), R("of3", c0, c1), "a")
+        else:
+            gather(wide("dd", c0, c1), full(key), R("far", c0, c1), "a", 0.25)
+
+    def s_open(kind, p, banks):
+        for h in banks:
+            c0, c1 = chunk(p, h)
+            if kind == "t":
+                mm(full(banks[h]), [(full("e256"), wide("mk", c0, c1))], True, False)
+            else:
+                mm(full(banks[h]), [(full("e0"), R("pm", 0, CH))], True, False)
+                for i in range(16):
+                    mm(R(banks[h], i, CH, 16), [(full("en"), R("xq", c0, c1))], False, False)
+
+    def s_piece(kind, key, p, banks):
+        for h in banks:
+            s_gather(kind, key, p, h)
+        for h in banks:
+            c0, c1 = chunk(p, h)
+            mm(full(banks[h]), [(full("e1" if kind == "t" else "e4"), wide("dd", c0, c1))], False, True)
+            urgent[len(tasks) - 1] = SU
+            posts.append(len(tasks) - 1)
+            if kind == "t":
+                act(wide("gb", c0, c1), full(banks[h]), Fn.Relu, bias=-256.0)
+            else:
+                act(wide("gb", c0, c1), full(banks[h]), Fn.Abs)
+
+    XB = ({0: "sca", 1: "scb"}, {0: "da", 1: "db"}, {0: "wa", 1: "wb"})
+    posts = []
+
+    def t_banks(t, p):
+        return {c % 2: TBK[n] for n, c in enumerate(TS[t]) if c // 2 == p}
+
+    def open_x(t):
+        for p in range(ND[t]):
+            s_open("x", p, XB[p])
+
+    def open_t(t):
+        for p in range(NP):
+            s_open("t", p, t_banks(t, p))
+
+    def rn(o, c0, c1):
+        mm(o, [(R("zr", 15 - i, 143 - i), R("gb", 16 * c0 + i, 16 * c1, 16)) for i in range(16)])
 
     def r2(p):
-        name, c = ("r2a", "r2b")[p // 2 % 2], p % 2 * PV
+        name, c = ("ra", "rb")[p // 2 % 2], p % 2 * PV
         for ih in (0, 1):
             mm(R(name, ih * 128 + c, ih * 128 + c + PV),
                [(R("z2", 7 - i, 135 - i), R("gb", p * PW + 8 * ih + i, (p + 1) * PW, 16)) for i in range(8)])
 
-    def r2copy(part):
-        for ih in (0, 1):
-            copy(wat(part, 8 * ih, 8 * ih + 1), R(("r2a", "r2b")[part % 2], ih * 128, (ih + 1) * 128), "a")
+    def sums(part, z, at):
+        name, to = ("ra", "rb")[part % 2], R("aa", part % 2 * 256, part % 2 * 256 + 256)
+        for i in range(16):
+            mm(R(name, *at(i)), [(R("gb", 2 * part * PW + i, 2 * (part + 1) * PW, 16), full(z))])
+        copy(to, R(name, 0, 256), "a")
+        return name, to[1]
 
-    def rn2(part):
-        mm(R(("rna", "rnb")[part % 2], 0, 128), [(R("z3", 8 - 8 * ih, 136 - 8 * ih), wat(part, 8 * ih, 8 * ih + 1)) for ih in (0, 1)])
+    def r2s(part):
+        name, c = sums(part, "z6", lambda i: (i // 8 * 128 + i % 8, i // 8 * 128 + 128, 8))
+        for ih in (0, 1):
+            mm(R(name, 256 + ih * 128, 384 + ih * 128), [(R("aa", c + ih * 128, c + ih * 128 + 128), full("e1"))])
+        r2copy(part, 256)
+
+    def r2copy(part, c=0):
+        for ih in (0, 1):
+            copy(wat(part, 8 * ih, 8 * ih + 1), R(("ra", "rb")[part % 2], c + ih * 128, c + (ih + 1) * 128), "a")
+
+    def rn2_bank(part):
+        c = 0 if part in STAT else 256
+        return R(("ra", "rb")[part % 2], c, c + 128)
+
+    def rn2(part, o=None, z="z3"):
+        mm(o or rn2_bank(part), [(R(z, 8 - 8 * ih, 136 - 8 * ih), wat(part, 8 * ih, 8 * ih + 1)) for ih in (0, 1)])
 
     def far(part):
-        src = R(("rna", "rnb")[part % 2], 0, 128)
-        ts(R("far", part * 128, (part + 1) * 128), src, -7.5, Op.add, 0.0625, Op.mult)
-        copy(R("rs", part * 128, (part + 1) * 128), src, "a")
+        ts(R("far", part * 128, (part + 1) * 128), rn2_bank(part), -7.5, Op.add, 0.0625, Op.mult)
 
-    def rs(p):
-        copy(R("rs", p * PV, (p + 1) * PV), rn_bank(p), "a")
+    def rs2(part):
+        copy(R("rs", part * 128, (part + 1) * 128), rn2_bank(part), "a")
 
     def x_gather(key, c0, c1):
-        tt(R("dd", 16 * c0, 16 * c1), full(key), R("xr", 16 * c0, 16 * c1), Op.subtract, off=R("far", c0, c1))
+        tt(wide("dd", c0, c1), full(key), wide("xr", c0, c1), Op.subtract, off=R("far", c0, c1))
+        in_turn("vx")
 
     def absd(c0, c1):
-        o, i = R("gb", 16 * c0, 16 * c1), R("dd", 16 * c0, 16 * c1)
-        op("a", lambda: A_.activation(ap(o), ap(i), Fn.Abs), [i], [o])
+        act(wide("gb", c0, c1), wide("dd", c0, c1), Fn.Abs)
 
-    def score(p, s0=0, s1=16):
-        o = R("sca", p * PV, (p + 1) * PV) if p < NP - 1 else R("scb", 0, PV)
-        mm(o, [(R("zs", 15 - s, 143 - s), R("gb", p * PW + 64 * s, p * PW + 64 * (s + 1))) for s in range(s0, s1)],
-           s0 == 0, s1 == 16)
+    def relu(c0, c1):
+        ts(wide("gb", c0, c1), wide("dd", c0, c1), 0.0, Op.max)
 
-    def scan(c0, c1, src):
-        o, d = R("sc", c0, c1), R("d0", c0, c1)
-        op("v", lambda: V_.tensor_tensor_scan(ap(o), ap(d), ap(src), 0.0, Op.add, Op.max), [d, src], [o])
+    def score(p, o, s0=0, s1=16, from_relu=False):
+        run = lambda n, s: R(n, p * PW + 64 * s, p * PW + 64 * (s + 1))
+        if from_relu:
+            pairs = [(R("zn", 15 - s, 143 - s), run("dd", s)) for s in range(s0, s1)]
+            pairs += [(R("zp", 15 - s, 143 - s), run("gb", s)) for s in range(s0, s1)]
+        else:
+            pairs = [(R("zs", 15 - s, 143 - s), run("gb", s)) for s in range(s0, s1)]
+        mm(o, pairs, s0 == 0, s1 == 16)
 
-    def lists():
-        ts(full("rj"), full("ri"), 7, Op.bitwise_and)
-        ts(full("of3"), full("ri"), -3.5, Op.add, 0.125, Op.mult)
-        copy(full("jl"), full("rj"))
+    def scan(p0, p1, src):
+        o, d = R("sc", p0 * PV, p1 * PV), R("d0", p0 * PV, p1 * PV)
+        op("v", lambda: V_.tensor_tensor_scan(ap(o), ap(d), ap(src), 0.0, Op.add, Op.max), [d, src], [o], size(o))
 
-    def mask(p):
-        gather(R("mk", p * PW, (p + 1) * PW), full("em"), R("jl", p * PV, (p + 1) * PV), "a")
+    def sca(p0, p1=None):
+        return R("sca", p0 * PV, (p1 or p0 + 1) * PV)
 
-    def xrep(key, on_a=0):
-        gather(full("xq"), own(key), full("vq"))
-        for i in range(on_a):
-            copy(R("xr", i, 6144, 16), full("xq"), "a")
-        return [lambda i=i: copy(R("xr", i, 6144, 16), full("xq")) for i in range(on_a, 16)]
-
-    def x_phase(t, extra):
-        key = "x%d" % (t - 1)
-        for p in range(NP):
-            if p < NP - 1:
-                x_gather(key, p * PV, (p + 1) * PV)
-            else:
-                x_gather(key, p * PV, p * PV + 32)
-                x_gather(key, p * PV + 32, p * PV + 48)
-                x_gather(key, p * PV + 48, p * PV + 64)
-            for f in extra[p][0]:
-                f()
-            if p >= 1:
-                absd((p - 1) * PV, p * PV)
-                score(p - 1)
-            for f in extra[p][1]:
-                f()
-        c = (NP - 1) * PV
-        absd(c, c + 32)
-        score(NP - 1, 0, 8)
-        absd(c + 32, c + 48)
-        score(NP - 1, 8, 12)
-        absd(c + 48, c + 64)
-        score(NP - 1, 12, 16)
-        scan(0, c, R("sca", 0, c))
+    def mask_list(t):
         if t == 3:
-            gather(full("ri"), full("rs"), full("qv"))
-        elif t == 2:
-            copy(full("ri"), full("rs"))
-        scan(c, V, R("scb", 0, PV))
+            copy(full("lo"), R("db", 0, V), "a")
+            gather(full("jl"), full("lo"), full("qv"))
+        else:
+            copy(full("jl"), full("rk") if t == 1 else R("db", 0, V))
+
+    def t_list(t):
+        if t == 3:
+            copy(full("rs"), R("da", 0, V), "a")
+            ts(full("of3"), full("rs"), -3.5, Op.add, 0.125, Op.mult, off=full("qv"))
+        else:
+            ts(full("of3"), full("ri") if t == 1 else R("da", 0, V), -3.5, Op.add, 0.125, Op.mult)
+
+    def mask(p, e="a"):
+        for h in (0, 1):
+            c0, c1 = chunk(p, h)
+            gather(wide("mk", c0, c1), full("em"), R("jl", c0, c1), e)
+
+    def xrep(key, nd, on_a=0, on_g=0):
+        o, src = own(key), R("xq", nd * PV, V)
+        gather(full("xq"), o, full("vq"))
+        for i in range(on_a):
+            copy(R("xr", nd * PW + i, 6144, 16), src, "a")
+        for i in range(on_a, on_a + on_g):
+            to = R("xr", nd * PW + i, 6144, 16)
+            op("g", lambda to=to: g.affine_select(ap(to), ap(src), [[0, size(src)]], Op.is_ge, 0.0, 0, 0), [src], [to], 200 + 2 * size(src))
+            in_turn("send")
+        on_a += on_g
+        return ([lambda i=i: copy(R("xr", nd * PW + i, 6144, 16), src) for i in range(on_a, 16)]
+                + [lambda: ts(R("zz", 0, nd * PV), R(key, o[1], o[1] + nd * PV), 0.75, Op.mult, -0.375, Op.add)] * (nd > 0))
+
+    def v_piece(key, p, post):
+        x_gather(key, p * PV, (p + 1) * PV)
+        if post == "v":
+            relu(p * PV, (p + 1) * PV)
+
+    def v_last(key, p, on_a):
+        c = p * PV
+        for a, b in ((0, 32), (32, 48), (48, 64)):
+            x_gather(key, c + a, c + b)
+            (absd if on_a else relu)(c + a, c + b)
+            score(p, R("scb", 0, PV), a // 4, b // 4, not on_a)
 
     def tail(t):
-        tk = "t%d" % t
-        keys = R("sc", 15, V, 16)
+        tk, nd = "t%d" % t, ND[t]
+        keys, begin = R("sc", 15, V, 16), len(tasks)
         copy(full("ki"), keys)
         ts(full("par"), full("ki"), 1, Op.bitwise_and)
         copy(full("parf"), full("par"))
         mm(R("sca", 0, 24), [(full("ones"), full("parf"))])
+        urgent[len(tasks) - 1] = 3
         ts(full("kk"), full("ki"), 15, Op.bitwise_and)
         op("v", lambda: V_.tensor_reduce(ap(col("ss", 0)), ap(R("sca", 0, 24)), AxisListType.X, Op.add),
-           [R("sca", 0, 24)], [col("ss", 0)])
+           [R("sca", 0, 24)], [col("ss", 0)], 64)
         ts(full("tt"), keys, col("ss", 0), Op.add, 1.0, Op.add)
         ts(full("yy"), full("tt"), 15, Op.bitwise_and)
         ts(full("a0"), full("yy"), 1.0, Op.max, 128.0, Op.mult)
@@ -356,29 +551,48 @@ def rank_program(g, core, T, topo):
         copy(full("u0"), full("o0"))
         tt(full("o1"), full("o0"), full("ee"), Op.add)
         o = own(tk)
-        gather(R(tk, o[1], o[2], 2), full("ww"), full("u0"), "a")
+        for z, bank in (("z5", "db"), ("z3", "da")) if t > 1 else ():
+            for part in range(3):
+                rn2(part, R(bank, 128 * part, 128 * (part + 1)), z)
+                turns["rn%d%s%d" % (t, z, part)] = [begin + 3, len(tasks) - 1]
+                urgent[len(tasks) - 1] = 0
         ts(full("u1"), full("o1"), -1024.0, Op.add)
-        gather(R(tk, o[1] + 1, o[2], 2), full("ww"), full("u1"))
+        for h in range(TCUT):
+            a, b = h * 24 // TCUT, (h + 1) * 24 // TCUT
+            gather(R(tk, o[1] + 32 * a, o[1] + 32 * b, 2), full("ww"), R("u0", a, b), "a")
+            gather(R(tk, o[1] + 32 * a + 1, o[1] + 32 * b, 2), full("ww"), R("u1", a, b))
+        gate = len(tasks) - 1
+        for i in range(begin, len(tasks)):
+            urgent.setdefault(i, 1)
         send(tk)
-        if t > 1:
-            lists()
+        mask_list(t)
         tt(full("ox"), full("c16"), full("kk"), Op.subtract)
         copy(full("oxu"), full("ox"))
-        ts(full("dq"), full("dd"), -1.5, Op.add, 0.25, Op.mult, off=full("oxu"))
+        c = nd * PV
+        old = own("x%d" % (t - 1))
         nxt = own("x%d" % t) if t < 3 else full("xo")
-        tt(nxt, full("dq"), own("x%d" % (t - 1)), Op.add)
+        if c:
+            tt(R("dq", 0, c), full("dd"), R("zz", 0, c), Op.add, off=R("oxu", 0, c // 16))
+            copy(R(nxt[0], nxt[1], nxt[1] + c), R("dq", 0, c))
+        ts(R("dq", c, V), full("dd"), -1.5, Op.add, 0.25, Op.mult, off=R("oxu", c // 16, V // 16))
+        tt(R(nxt[0], nxt[1] + c, nxt[2]), R("dq", c, V), R(old[0], old[1] + c, old[2]), Op.add)
         if t < 3:
             send("x%d" % t)
         else:
-            op("s", lambda: g.sync.dma_start(T.yx[:], ap(nxt)), [nxt], [], sem="st")
+            dma("s", T.yx[:], ap(nxt), [nxt], [], "st")
+        rest = xrep("x%d" % t, ND[t + 1], 0, XG) if t < 3 else []
+        t_list(t)
         for p in range(NP):
-            mask(p)
+            mask(p, MENG[t][p].replace("x", "any"))
+        for f in rest:
+            f()
+        open_t(t)
         if t < 3:
-            for f in xrep("x%d" % t):
-                f()
+            open_x(t + 1)
+        gates[gate] = len(tasks)
 
-    op("s", lambda: g.sync.dma_start(ap(own("x0")), T.x[:]), [], [own("x0")], sem="ldx")
-    op("a", lambda: g.scalar.dma_start(ap(full("rin")), T.rot[:]), [], [full("rin")], sem="ldr")
+    dma("s", ap(own("x0")), T.x[:], [], [own("x0")], "ldx")
+    dma("a", ap(full("rin")), T.rot[:], [], [full("rin")], "ldr")
     iota(col("pid", 0), [[0, 1]], 0, 1)
     iota(full("vq0"), [[64, 6], [4, 4]], 0, 0)
     iota(full("ci"), [[1, 144]], -15, 0)
@@ -398,69 +612,127 @@ def rank_program(g, core, T, topo):
             ts(col("pi", c), col("pid", 0), mk, Op.bitwise_and)
     fill(R("d0", 0, V, 16), -1.0e6)
     copy(full("pf"), full("pi"))
+    copy(col("pc", 5), col("pid", 0))
     ts(col("pc", 0), col("pf", 5), 16.0, Op.mult, col("pf", 6), Op.add)
     ts(col("pc", 1), col("pf", 4), 0.125, Op.mult)
     ts(col("pc", 2), col("pf", 4), -0.125, Op.mult, 1.0, Op.add)
     ts(full("vq"), full("vq0"), col("pc", 0), Op.add)
     ts(R("z40", 0, 136), R("ci", 7, 143), col("pf", 2), Op.is_equal, col("pc", 2), Op.mult)
     ts(R("z41", 0, 136), R("ci", 7, 143), col("pf", 2), Op.is_equal, col("pc", 1), Op.mult)
-    rest = xrep("x0", 5)
     gather(full("ri"), full("rin"), full("vq"))
     ts(full("rj"), full("ri"), 8, Op.logical_shift_right)
     ts(full("rk"), full("ri"), 255, Op.bitwise_and)
     copy(full("hi"), full("rj"))
     copy(full("lo"), full("rk"))
-    for ih, name in ((0, "r2a"), (1, "r2b")):
+    for ih, name in ((0, "ra"), (1, "rb")):
         z = "z4%d" % ih
         mm(R(name, 0, V), [(R(z, 8, 136), full("hi")), (R(z, 0, 128), full("lo"))])
         for part in range(3):
             copy(wat(part, 8 * ih, 8 * ih + 1), R(name, 128 * part, 128 * (part + 1)), "a")
     ts(full("far"), full("ri"), -7.5, Op.add, 0.0625, Op.mult)
-    for f in rest:
+    for z, w in (("e4", 4.0), ("en", -1.0), ("e0", 0.0)):
+        ts(full(z), R("ci", 15, 143), col("pc", 5), Op.is_equal, w, Op.mult)
+    for f in xrep("x0", ND[1], 0, XG0):
         f()
+    open_x(1)
     for part in range(3):
-        for f in w_half(part, 0) + w_half(part, 1):
-            f()
-    ts(R("zs", 0, 143), R("ci", 0, 143), col("pf", 0), Op.is_equal, 16.0, Op.mult)
+        w_half(part, 0, "any")
+        w_half(part, 1, "any")
+    for z, w in (("zs", 16.0), ("zp", 32.0), ("zn", -16.0)):
+        ts(R(z, 0, 143), R("ci", 0, 143), col("pf", 0), Op.is_equal, w, Op.mult)
     ts(col("pc", 3), col("pf", 7), 4.0, Op.mult)
     ts(col("pc", 4), col("pf", 4), -31.875, Op.mult, 256.0, Op.add)
-    ts(full("em"), R("ci", 15, 31), col("pf", 3), Op.is_equal)
+    iota(full("em0"), [[0, 32], [1, 8]], 0, 0)
+    ts(full("em"), full("em0"), col("pf", 3), Op.is_equal)
     ts(full("qb"), full("qb0"), col("pc", 3), Op.add)
     ts(full("qw"), full("qw0"), col("pc", 3), Op.add)
     ts(full("c16"), full("qb"), 16.0, Op.mult, 15.0, Op.add)
     copy(full("qv"), full("qb"))
-    lists()
-
-    x_phase(1, [([], [])] * NP)
-    tail(1)
+    ts(col("pj", 0), col("pid", 0), 3, Op.logical_shift_right)
+    ts(col("pj", 1), col("pid", 0), 4, Op.logical_shift_right)
+    ts(col("pc", 7), col("pj", 1), col("pf", 4), Op.add)
+    copy(col("pc", 6), col("pj", 0))
+    ts(full("z6"), R("ci", 15, 31), col("pc", 6), Op.is_equal)
+    ts(full("z7"), R("ci", 15, 31), col("pc", 7), Op.is_equal)
+    ts(R("z5", 0, 136), R("ci", 7, 143), col("pf", 2), Op.is_equal, col("pc", 1), Op.mult)
     ts(R("zr", 0, 143), R("ci", 0, 143), col("pf", 0), Op.is_equal, col("pc", 4), Op.mult)
     ts(R("z3", 0, 136), R("ci", 7, 143), col("pf", 2), Op.is_equal, col("pc", 4), Op.mult)
     ts(R("z2", 0, 135), R("ci", 8, 143), col("pf", 1), Op.is_equal)
+    for z, w in (("e1", 1.0), ("e256", 256.0)):
+        ts(full(z), R("ci", 15, 143), col("pc", 5), Op.is_equal, w, Op.mult)
+
+    def x_phase(t):
+        key, nd = "x%d" % (t - 1), ND[t]
+        for p in XORD[t]:
+            bank = R("ra", 0, PV) if p == nd - 1 and XORD[t].index(p) > 3 else R("scb", 0, PV) if p == NP - 1 else R("sca", p * PV, (p + 1) * PV)
+            if p < nd:
+                s_piece("x", key, p, XB[p])
+                score(p, bank)
+            elif p == NP - 1:
+                v_last(key, p, p in ABS[t])
+            else:
+                x_gather(key, p * PV, (p + 1) * PV)
+                (absd if p in ABS[t] else relu)(p * PV, (p + 1) * PV)
+                score(p, bank, from_relu=p not in ABS[t])
+            scan(p, p + 1, bank)
+
+    def t_piece(t, p):
+        banks = t_banks(t, p)
+        s_piece("t", "t%d" % t, p, banks)
+        mine = [chunk(p, h) for h in (0, 1) if h not in banks]
+        if mine:
+            t_gather("t%d" % t, mine[0][0], mine[-1][1])
+
+    x_phase(1)
+    tail(1)
 
     for t in (2, 3):
-        tk = "t%d" % (t - 1)
+        fars = []
         for p in range(NP):
-            t_gather(tk, p)
-            if p >= 2:
-                for f in w_half(p // 2 - 1, p % 2):
-                    f()
-            if p in (3, 5):
-                far(p // 2 - 1)
-            r2(p)
+            t_piece(t - 1, p)
+            begin = len(tasks)
+            if p // 2 not in STAT:
+                r2(p)
             if p % 2:
-                r2copy(p // 2)
+                (r2s if p // 2 in STAT else r2copy)(p // 2)
                 rn2(p // 2)
-        x_phase(t, [(w_half(2, 0), []), (w_half(2, 1) + [lambda: far(2)], [])] + [([], [])] * 4)
+                far(p // 2)
+                fars.append(len(tasks) - 1)
+            urgent.update((i, FU) for i in range(begin, len(tasks)))
+        if FAR0:
+            turns["far%d" % t] = [last_t[FAR0], fars[0]]
+        del last_t[:]
+        x_phase(t)
+        last_abs = max(i for i, x in enumerate(tasks) if x[0] == "a")
+        for n in range(6):
+            w_half(n // 2, n % 2, WENG[n].replace("x", "any"))
+            if n == WLATE:
+                turns["w%d" % t] = [last_abs, len(tasks) - 2]
         tail(t)
 
-    cuts = {2: 0, 4: 3 * PV, 5: 5 * PV}
+    def finish(p):
+        bank = R(("ra", "scb")[p % 2], 0, PV)
+        rn(bank, p * PV, (p + 1) * PV)
+        copy(R("rs", p * PV, (p + 1) * PV), bank, "any" if p == NP - 1 else "a")
+
+    def store(p0, p1):
+        a, b = p0 * PV, p1 * PV
+        dma("s", T.yr[:, a:b], ap(R("rs", a, b)), [R("rs", a, b)], [], "st")
+
     for p in range(NP):
-        t_gather("t3", p)
-        rn(p)
-        rs(p)
-        if p in cuts:
-            a, b = cuts[p], (p + 1) * PV
-            op("s", lambda: g.sync.dma_start(T.yr[:, a:b], ap(R("rs", a, b))), [R("rs", a, b)], [], sem="st")
+        t_piece(3, p)
+        if p // 2 not in STAT3:
+            finish(p)
+        elif p % 2:
+            name, c = sums(p // 2, "z7", lambda i: (i, 256, 16))
+            mm(R(name, 256, 384), [(R("aa", c, c + 128), full("e256")), (R("aa", c + 128, c + 256), full("e1"))])
+            copy(R("rs", (p - 1) * PV, (p + 1) * PV), R(name, 256, 384), "a")
+        if p in (3, 5):
+            store(0 if p == 3 else 4, p + 1)
+    if not ORDER:
+        ORDER.extend(order())
+    for i, e in ORDER:
+        issue(*[t for t in [tasks[i]] + other.get(i, []) if t[0] == e][0])
     g.sync.wait_ge(T.sem.st, count["st"])
     g.wait_ge(T.sem.sent, sent[0])
     for s in ("sv", "sa", "sp", "sg"):

from concourse.bass import DstId, RemoteDMATransfer
from concourse.mybir import AluOpType as Op, AxisListType, ActivationFunctionType as Fn

NR, V, NP, PV = 8, 384, 6, 64
PW = 16 * PV
CH = PW // 2
ND = {1: 1, 2: 1, 3: 1}
ABS = {t: range(NP) for t in (1, 2, 3)}
TS = {1: (2, 3), 2: (2, 3), 3: (3, 6, 7)}
WENG = "aaxxxx"
MENG = {1: "xxxxxx", 2: "xxxxxx", 3: "xxxxxx"}
SU = 2
WLATE = 9
TBK = ("wa", "wb", "da", "db", "sca")
FAR0 = 0
XG = 12
XG0 = 8
FU = 3
WB = ("da", "db", "wa", "wb")
STAT = (0, 1, 2)
STAT3 = (0, 1)
XORD = {1: (0, 1, 2, 3, 4, 5), 2: (0, 1, 2, 3, 4, 5), 3: (0, 1, 2, 3, 4, 5)}
WU = 0
TCUT = 2
T_LANES = ((None, 0, 2, 0, 4), (1, 0, 2, 4, 7), (2, 1, 2, 4, 7), (0, 1, 2, 1, 4), (None, 1, 2, 0, 1))
X_LANES = ((1, 0, 1, 0, 2), (2, 0, 1, 2, 4), (0, 0, 1, 4, 7))
X0_LANES = ((None, 0, 1, 0, 4), (1, 0, 1, 4, 5), (2, 0, 1, 5, 6), (0, 0, 1, 6, 7))
PLAN = {"x0": X0_LANES, "t1": T_LANES, "x1": X_LANES, "t2": T_LANES, "x2": X_LANES, "t3": T_LANES}
FIX, LOCAL = 60, 2600
WAKE = 140
SLACK = 100
FUSED = 1.56
AFIX = 60
GATHER = 1.56
COLUMN = 1.0
EXCHANGE = {"x0": 10000, "t1": 8000, "x1": 9500, "t2": 8000, "x2": 9500, "t3": 8000}

BF, F32, I32, U16 = "bfloat16", "float32", "int32", "uint16"
SCRATCH = {}
for _n, _w, _d in [
    ("x0", 3072, BF), ("x1", 3072, BF), ("x2", 3072, BF), ("t1", 6144, BF), ("t2", 6144, BF), ("t3", 6144, BF),
    ("gb", 6144, BF), ("dd", 6144, BF), ("mk", 6144, BF), ("xr", 6144, BF), ("ww", 6144, BF),
    ("xo", 384, BF), ("xq", 384, BF), ("hi", 384, BF), ("lo", 384, BF), ("rin", 384, I32), ("rs", 384, F32),
    ("ri", 384, I32), ("rj", 384, I32), ("rk", 384, I32), ("dq", 384, I32), ("sc", 384, F32), ("d0", 384, F32),
    ("zz", 384, F32), ("far", 384, U16), ("of3", 384, U16), ("jl", 384, U16),
    ("pid", 8, I32), ("pi", 8, I32), ("pf", 8, F32), ("pc", 8, F32), ("ci", 144, F32),
    ("vq0", 24, I32), ("qb0", 24, I32), ("qw0", 24, I32), ("qw", 24, F32), ("vq", 24, U16), ("qv", 24, U16), ("qb", 24, F32), ("c16", 24, F32),
    ("ki", 24, I32), ("par", 24, I32), ("parf", 24, BF), ("kk", 24, I32), ("ox", 24, F32), ("oxu", 24, U16),
    ("ss", 8, F32), ("tt", 24, I32), ("yy", 24, I32), ("a0", 24, F32), ("ee", 24, F32), ("o0", 24, F32), ("o1", 24, F32),
    ("u0", 24, U16), ("u1", 24, U16),
    ("ones", 128, BF), ("zs", 144, BF), ("zp", 144, BF), ("zn", 144, BF), ("zr", 144, BF), ("z2", 144, BF), ("z3", 144, BF),
    ("z40", 144, BF), ("z41", 144, BF), ("e1", 128, BF), ("e4", 128, BF), ("e0", 128, BF), ("en", 128, BF), ("e256", 128, BF),
    ("em", 256, BF), ("em0", 256, BF), ("z5", 144, BF), ("z6", 16, BF), ("z7", 16, BF), ("aa", 512, BF), ("pj", 8, I32), ("pm", 896, BF),
]:
    SCRATCH[_n] = ("sbuf", [128, _w], _d)
PS = ["ra", "rb", "da", "db", "wa", "wb", "sca", "scb"]
for _n in PS:
    SCRATCH[_n] = ("psum", [128, 512], F32)
SEMAPHORES = ["sv", "sa", "sp", "sg", "ldx", "ldr", "st", "sent"] + ["ar_" + k for k in PLAN]
ORDER = []


def R(name, lo, hi, step=1):
    return (name, lo, hi, step)


def clash(a, b):
    if a[0] != b[0] or a[1] >= b[2] or b[1] >= a[2]:
        return False
    return not (a[3] > 1 and a[3] == b[3] and (a[1] - b[1]) % a[3] != 0)


def peers_of(T, rank):
    return [T.cores[(rank + d) % NR] for d in range(1, NR)]


def helpers_of(topo, c):
    near = [h for h in topo.cores_of(c) if h != c and topo.die(h) == topo.die(c)]
    far = [h for h in topo.cores_of(c) if topo.die(h) != topo.die(c)]
    return [near[0], far[0], far[1]]


def bits(m):
    return bin(m).count("1")


def dst_id(topo, d, s):
    rid, pid = topo.addr(d, s)
    return DstId(rid=rid, pnc=pid)


def part_of(T, key, rank, part, parts):
    w = T[key].shape[1] // NR
    return rank * w + part * w // parts, rank * w + (part + 1) * w // parts


def hop_mask(topo, rc, peer, helper):
    return topo.mask(rc, helper) & ~topo.mask(rc, peer)


def helper_program(g, core, T, topo):
    own = [c for c in topo.cores_of(core) if T.rank_of(c) is not None]
    if not own:
        return
    rc = own[0]
    rank = T.rank_of(rc)
    hs = helpers_of(topo, rc)
    if core not in hs:
        return
    peers = peers_of(T, rank)
    sent = 0
    for key, lanes in PLAN.items():
        for who, part, parts, p0, p1 in lanes:
            if who != hs.index(core):
                continue
            a, b = part_of(T, key, rank, part, parts)
            g.wait_ge(T.sem["ar_" + key], bits(hop_mask(topo, rc, peers[0], core)))
            m = topo.mask(core, peers[p0])
            g.remote_dma_fused([RemoteDMATransfer(dst_ids=[dst_id(topo, d, core) for d in peers[p0:p1]], dma_engine_mask=m,
                                                  remote_sem=T.sem["ar_" + key], srcs=[T[key][:, a:b]],
                                                  dsts=[T[key][:, a:b] for d in peers[p0:p1]])], local_sem=T.sem.sent)
            sent += bits(m)
    if sent:
        g.wait_ge(T.sem.sent, sent)


def rank_program(g, core, T, topo):
    rank = T.rank_of(core)
    if rank is None:
        helper_program(g, core, T, topo)
        return
    Q = {"v": g.vector, "a": g.scalar, "p": g.tensor, "g": g, "s": g.sync}
    SEM = {"v": "sv", "a": "sa", "p": "sp", "g": "sg"}
    count = {}
    known = {e: {} for e in Q}
    clock = {}
    log = []

    def ap(r):
        return T[r[0]][:, r[1]:r[2]] if r[3] == 1 else T[r[0]][:, r[1]:r[2]:r[3]]

    def ind(win, off):
        return ap(win).indirect(ap(off))

    def wait(e, tok):
        if known[e].get(tok[0], 0) >= tok[1]:
            return
        Q[e].wait_ge(T.sem[tok[0]], tok[1])
        for s, n in clock[tok].items():
            known[e][s] = max(known[e].get(s, 0), n)

    def deps(e, reads, writes):
        need = {}
        for reg, w, oe, tok in log:
            if oe == e and e == "p":
                continue
            hit = False
            if reg[0] in PS and oe != e:
                hit = any(r[0] == reg[0] for r in reads + writes)
            else:
                hit = any(clash(reg, r) for r in writes) or (w and any(clash(reg, r) for r in reads))
            if hit:
                need[tok[0]] = max(need.get(tok[0], 0), tok[1])
        toks = sorted(need.items(), key=lambda t: -len(clock[t]))
        for t in toks:
            wait(e, t)

    def note(e, tok, reads, writes, ck):
        clock[tok] = dict(ck)
        clock[tok][tok[0]] = tok[1]
        for r in reads:
            log.append((r, False, e, tok))
        for r in writes:
            log.append((r, True, e, tok))

    tasks, other, turns, gates, urgent = [], {}, {}, {}, {}

    def op(e, fn, reads, writes, cost, sem=None, late=0, landed=None):
        tasks.append((e, fn, reads, writes, cost, sem, late, landed))

    def issue(e, fn, reads, writes, cost, sem, late, landed):
        if landed is not None:
            deps(e, reads, [])
            fn()
            note("dma", landed, [], writes, {})
            return
        deps(e, reads, writes)
        s, n = (SEM[e], 1) if sem is None else (sem, 16)
        fn().then_inc(T.sem[s], n)
        count[s] = count.get(s, 0) + n
        note(e if sem is None else "dma", (s, count[s]), reads, writes, known[e])

    def order():
        n = len(tasks)
        before, seen = [set() for _ in range(n)], {}
        for i, t in enumerate(tasks):
            for regs, w in ((t[2], False), (t[3], True)):
                for r in regs:
                    before[i].update(j for q, qw, j in seen.get(r[0], ()) if (w or qw) and clash(q, r))
            for regs, w in ((t[2], False), (t[3], True)):
                for r in regs:
                    seen.setdefault(r[0], []).append((r, w, i))
        for row in turns.values():
            for a, b in zip(row, row[1:]):
                before[b].add(a)
        after = [[] for _ in range(n)]
        for i in range(n):
            before[i].update(j for j in gates if j < i and tasks[i][0] in "vap" and i < gates[j])
            for j in before[i]:
                after[j].append(i)
        left, ready, free, bank = [len(b) for b in before], [0.0] * n, {e: 0.0 for e in Q}, {}
        cand, out = {i for i in range(n) if not left[i]}, []
        banks = [{r[0] for r in t[2] + t[3] if r[0] in PS} for t in tasks]

        def start(i, e):
            return max([ready[i], free[e]] + [bank[b][1] + WAKE for b in banks[i] if b in bank and bank[b][0] != e])
        while cand:
            st = {(i, t[0]): (start(i, t[0]), t) for i in cand for t in [tasks[i]] + other.get(i, [])}
            first = min(st, key=lambda k: (st[k][0], k))
            e = first[1]
            k = min((k for k in st if k[1] == e and st[k][0] <= st[first][0] + SLACK), key=lambda k: (-urgent.get(k[0], 0), k))
            i, t = k[0], st[k][1]
            cand.remove(i)
            out.append(k)
            free[e] = st[k][0] + t[4]
            for b in banks[i]:
                bank[b] = (e, free[e])
            for j in after[i]:
                linked = (e, tasks[j][0]) != ("p", "p") and any(clash(a, b) for a in t[2] + t[3] for b in tasks[j][2] + tasks[j][3])
                ready[j] = max(ready[j], free[e] + (t[6] + WAKE if linked else 0))
                left[j] -= 1
                if not left[j]:
                    cand.add(j)
        return out

    def in_turn(name):
        turns.setdefault(name, []).append(len(tasks) - 1)

    def either(f):
        f("v")
        alt = tasks.pop()
        f("a")
        other[len(tasks) - 1] = [alt]

    V_, A_ = g.vector, g.scalar
    size = lambda r: len(range(r[1], r[2], r[3]))
    short = lambda *rs: all(SCRATCH[r[0]][2] in (BF, U16) for r in rs)

    def cycles(o, i, off=None, rate=1.0):
        return FIX + (FUSED if rate > 1 else GATHER) * size(o) if off else max(64, rate * size(o) * (0.5 if short(o, i) else 1))

    def copy(o, i, e="v"):
        if e == "any":
            either(lambda e: copy(o, i, e))
        elif e == "v":
            op(e, lambda: V_.tensor_copy(ap(o), ap(i)), [i], [o], cycles(o, i))
        else:
            act(o, i, Fn.Copy)

    def act(o, i, fn, **kw):
        op("a", lambda: A_.activation(ap(o), ap(i), fn, **kw), [i], [o], AFIX + size(o))

    def gather(o, win, off, e="v", scale=1.0):
        if e == "any":
            either(lambda e: gather(o, win, off, e))
        elif e == "v":
            op(e, lambda: V_.tensor_copy(ap(o), ind(win, off)), [win, off], [o], cycles(o, win, off))
        else:
            op(e, lambda: A_.activation(ap(o), ind(win, off), Fn.Copy, scale=scale), [win, off], [o], cycles(o, win, off))

    def ts(o, i, s1, op0, s2=None, op1=None, off=None):
        rd = [i] + [s for s in (s1, s2, off) if isinstance(s, tuple)]
        a1 = ap(s1) if isinstance(s1, tuple) else s1
        a2 = ap(s2) if isinstance(s2, tuple) else s2
        src = ap(i) if off is None else ind(i, off)
        if op1 is None:
            op("v", lambda: V_.tensor_scalar(ap(o), src, a1, None, op0), rd, [o], cycles(o, i, off))
        else:
            op("v", lambda: V_.tensor_scalar(ap(o), src, a1, a2, op0, op1), rd, [o], cycles(o, i, off))

    def tt(o, i0, i1, alu, off=None):
        src = ap(i0) if off is None else ind(i0, off)
        op("v", lambda: V_.tensor_tensor(ap(o), src, ap(i1), alu), [i0, i1] + ([off] if off else []), [o], cycles(o, i0, off, 2))

    def fill(o, c):
        op("v", lambda: V_.memset(ap(o), c), [], [o], cycles(o, o))

    def mm(o, pairs, first=True, last=True):
        def fn():
            for n, (l, r) in enumerate(pairs):
                ins = g.tensor.matmul(ap(o), ap(l), ap(r), first and n == 0, last and n == len(pairs) - 1)
            return ins
        op("p", fn, [x for pr in pairs for x in pr], [o], COLUMN * len(pairs) * max(64, size(o)))

    peers = peers_of(T, rank)
    hs = helpers_of(topo, core)
    off_mask = topo.mask(core, peers[0])
    sent = [0]

    def own(key):
        w = T[key].shape[1] // NR
        return R(key, rank * w, (rank + 1) * w)

    def send(key):
        lanes = PLAN[key]
        parts = lanes[0][2]
        o = own(key)
        sem = T.sem["ar_" + key]
        total = bits(off_mask) * sum(p1 - p0 for who, pt, n, p0, p1 in lanes)
        for part in range(parts):
            mine = R(key, *part_of(T, key, rank, part, parts))
            src, trs = ap(mine), []
            to = [(hop_mask(topo, core, peers[0], hs[0]), [hs[who] for who, pt, n, p0, p1 in lanes if who is not None and pt == part])]
            to += [(off_mask, peers[p0:p1]) for who, pt, n, p0, p1 in lanes if who is None and pt == part]
            for m, cores in to:
                if cores:
                    trs.append(RemoteDMATransfer(dst_ids=[dst_id(topo, d, core) for d in cores], dma_engine_mask=m,
                                                 remote_sem=sem, srcs=[src], dsts=[src for d in cores]))
                    sent[0] += bits(m)
            last = part == parts - 1
            op("g", lambda trs=trs: g.remote_dma_fused(trs, local_sem=T.sem.sent), [mine],
               [R(key, 0, o[1]), R(key, o[2], T[key].shape[1])] if last else [],
               400, late=EXCHANGE[key] if last else 0, landed=("ar_" + key, total))
            in_turn("send")

    def dma(e, out, in_, reads, writes, sem):
        op(e, lambda: Q[e].dma_start(out, in_), reads, writes, 100, sem=sem, late=LOCAL)

    def iota(o, pat, base, cm):
        if SCRATCH[o[0]][2] == I32:
            op("g", lambda: g.iota(ap(o), pat, base, cm), [], [o], 160 + 2 * size(o))
        else:
            op("g", lambda: g.iota(ap(o), pat, base, cm, allow_small_or_imprecise_dtypes=True), [], [o], 160 + 2 * size(o))

    def perm(m):
        pats = {1: [[2, 64], [-1, 2]], 2: [[4, 32], [-2, 2], [1, 2]], 3: [[4, 32], [-1, 4]], 4: [[8, 16], [-4, 2], [1, 4]],
                6: [[8, 16], [-2, 4], [1, 2]], 7: [[8, 16], [-1, 8]]}
        c0 = 128 * (m - 1)
        if m in pats:
            parts = [(R("pm", c0, c0 + 128), R("ones", 0, 128), pats[m], m)]
        else:
            parts = [(R("pm", c0 + b, c0 + 128, 2), R("ones", 0, 64), [[8, 16], [-4, 2], [2, 2]], m - b) for b in (0, 1)]
        for o, i, pat, base in parts:
            op("g", lambda o=o, i=i, pat=pat, base=base: g.affine_select(ap(o), ap(i), pat, Op.is_equal, 0.0, base, -1),
               [i], [o], 200 + 2 * size(o))

    full = lambda n: R(n, 0, SCRATCH[n][1][1])
    col = lambda n, c: R(n, c, c + 1)
    wide = lambda n, c0, c1: R(n, 16 * c0, 16 * c1)

    def wat(part, b0, b1):
        return R("ww", 2048 * part + 128 * b0, 2048 * part + 128 * b1)

    WG = ((1, 5), (5, 8), (9, 13), (13, 16))

    def w_mm(part, n):
        for b in range(*WG[n]):
            m, c = 16 - b, 128 * (b - WG[n][0])
            src = (16 - (m & 8)) & 15
            mm(R(WB[n % len(WB)], c, c + 128), [(R("pm", 128 * ((m & 7) - 1), 128 * (m & 7)), wat(part, src, src + 1))])
            urgent[len(tasks) - 1] = WU

    def w_copy(part, n, e="a"):
        b0, b1 = WG[n]
        copy(wat(part, b0, b1), R(WB[n % len(WB)], 0, 128 * (b1 - b0)), e)

    def w_half(part, h, e="a"):
        w_mm(part, 2 * h)
        w_mm(part, 2 * h + 1)
        w_copy(part, 2 * h, e)
        w_copy(part, 2 * h + 1, e)

    last_t = []

    def t_gather(key, c0, c1):
        tt(wide("gb", c0, c1), full(key), wide("mk", c0, c1), Op.mult, off=R("of3", c0, c1))
        last_t.append(len(tasks) - 1)

    def chunk(p, h):
        return p * PV + h * PV // 2, p * PV + (h + 1) * PV // 2

    def s_gather(kind, key, p, h):
        c0, c1 = chunk(p, h)
        if kind == "t":
            gather(wide("dd", c0, c1), full(key), R("of3", c0, c1), "a")
        else:
            gather(wide("dd", c0, c1), full(key), R("far", c0, c1), "a", 0.25)

    def s_open(kind, p, banks):
        for h in banks:
            c0, c1 = chunk(p, h)
            if kind == "t":
                mm(full(banks[h]), [(full("e256"), wide("mk", c0, c1))], True, False)
            else:
                mm(full(banks[h]), [(full("e0"), R("pm", 0, CH))], True, False)
                for i in range(16):
                    mm(R(banks[h], i, CH, 16), [(full("en"), R("xq", c0, c1))], False, False)

    def s_piece(kind, key, p, banks):
        for h in banks:
            s_gather(kind, key, p, h)
        for h in banks:
            c0, c1 = chunk(p, h)
            mm(full(banks[h]), [(full("e1" if kind == "t" else "e4"), wide("dd", c0, c1))], False, True)
            urgent[len(tasks) - 1] = SU
            posts.append(len(tasks) - 1)
            if kind == "t":
                act(wide("gb", c0, c1), full(banks[h]), Fn.Relu, bias=-256.0)
            else:
                act(wide("gb", c0, c1), full(banks[h]), Fn.Abs)

    XB = ({0: "sca", 1: "scb"}, {0: "da", 1: "db"}, {0: "wa", 1: "wb"})
    posts = []

    def t_banks(t, p):
        return {c % 2: TBK[n] for n, c in enumerate(TS[t]) if c // 2 == p}

    def open_x(t):
        for p in range(ND[t]):
            s_open("x", p, XB[p])

    def open_t(t):
        for p in range(NP):
            s_open("t", p, t_banks(t, p))

    def rn(o, c0, c1):
        mm(o, [(R("zr", 15 - i, 143 - i), R("gb", 16 * c0 + i, 16 * c1, 16)) for i in range(16)])

    def r2(p):
        name, c = ("ra", "rb")[p // 2 % 2], p % 2 * PV
        for ih in (0, 1):
            mm(R(name, ih * 128 + c, ih * 128 + c + PV),
               [(R("z2", 7 - i, 135 - i), R("gb", p * PW + 8 * ih + i, (p + 1) * PW, 16)) for i in range(8)])

    def sums(part, z, at):
        name, to = ("ra", "rb")[part % 2], R("aa", part % 2 * 256, part % 2 * 256 + 256)
        for i in range(16):
            mm(R(name, *at(i)), [(R("gb", 2 * part * PW + i, 2 * (part + 1) * PW, 16), full(z))])
        copy(to, R(name, 0, 256), "a")
        return name, to[1]

    def r2s(part):
        name, c = sums(part, "z6", lambda i: (i // 8 * 128 + i % 8, i // 8 * 128 + 128, 8))
        for ih in (0, 1):
            mm(R(name, 256 + ih * 128, 384 + ih * 128), [(R("aa", c + ih * 128, c + ih * 128 + 128), full("e1"))])
        r2copy(part, 256)

    def r2copy(part, c=0):
        for ih in (0, 1):
            copy(wat(part, 8 * ih, 8 * ih + 1), R(("ra", "rb")[part % 2], c + ih * 128, c + (ih + 1) * 128), "a")

    def rn2_bank(part):
        c = 0 if part in STAT else 256
        return R(("ra", "rb")[part % 2], c, c + 128)

    def rn2(part, o=None, z="z3"):
        mm(o or rn2_bank(part), [(R(z, 8 - 8 * ih, 136 - 8 * ih), wat(part, 8 * ih, 8 * ih + 1)) for ih in (0, 1)])

    def far(part):
        ts(R("far", part * 128, (part + 1) * 128), rn2_bank(part), -7.5, Op.add, 0.0625, Op.mult)

    def rs2(part):
        copy(R("rs", part * 128, (part + 1) * 128), rn2_bank(part), "a")

    def x_gather(key, c0, c1):
        tt(wide("dd", c0, c1), full(key), wide("xr", c0, c1), Op.subtract, off=R("far", c0, c1))
        in_turn("vx")

    def absd(c0, c1):
        act(wide("gb", c0, c1), wide("dd", c0, c1), Fn.Abs)

    def relu(c0, c1):
        ts(wide("gb", c0, c1), wide("dd", c0, c1), 0.0, Op.max)

    def score(p, o, s0=0, s1=16, from_relu=False):
        run = lambda n, s: R(n, p * PW + 64 * s, p * PW + 64 * (s + 1))
        if from_relu:
            pairs = [(R("zn", 15 - s, 143 - s), run("dd", s)) for s in range(s0, s1)]
            pairs += [(R("zp", 15 - s, 143 - s), run("gb", s)) for s in range(s0, s1)]
        else:
            pairs = [(R("zs", 15 - s, 143 - s), run("gb", s)) for s in range(s0, s1)]
        mm(o, pairs, s0 == 0, s1 == 16)

    def scan(p0, p1, src):
        o, d = R("sc", p0 * PV, p1 * PV), R("d0", p0 * PV, p1 * PV)
        op("v", lambda: V_.tensor_tensor_scan(ap(o), ap(d), ap(src), 0.0, Op.add, Op.max), [d, src], [o], size(o))

    def sca(p0, p1=None):
        return R("sca", p0 * PV, (p1 or p0 + 1) * PV)

    def mask_list(t):
        if t == 3:
            copy(full("lo"), R("db", 0, V), "a")
            gather(full("jl"), full("lo"), full("qv"))
        else:
            copy(full("jl"), full("rk") if t == 1 else R("db", 0, V))

    def t_list(t):
        if t == 3:
            copy(full("rs"), R("da", 0, V), "a")
            ts(full("of3"), full("rs"), -3.5, Op.add, 0.125, Op.mult, off=full("qv"))
        else:
            ts(full("of3"), full("ri") if t == 1 else R("da", 0, V), -3.5, Op.add, 0.125, Op.mult)

    def mask(p, e="a"):
        for h in (0, 1):
            c0, c1 = chunk(p, h)
            gather(wide("mk", c0, c1), full("em"), R("jl", c0, c1), e)

    def xrep(key, nd, on_a=0, on_g=0):
        o, src = own(key), R("xq", nd * PV, V)
        gather(full("xq"), o, full("vq"))
        for i in range(on_a):
            copy(R("xr", nd * PW + i, 6144, 16), src, "a")
        for i in range(on_a, on_a + on_g):
            to = R("xr", nd * PW + i, 6144, 16)
            op("g", lambda to=to: g.affine_select(ap(to), ap(src), [[0, size(src)]], Op.is_ge, 0.0, 0, 0), [src], [to], 200 + 2 * size(src))
            in_turn("send")
        on_a += on_g
        return ([lambda i=i: copy(R("xr", nd * PW + i, 6144, 16), src) for i in range(on_a, 16)]
                + [lambda: ts(R("zz", 0, nd * PV), R(key, o[1], o[1] + nd * PV), 0.75, Op.mult, -0.375, Op.add)] * (nd > 0))

    def v_piece(key, p, post):
        x_gather(key, p * PV, (p + 1) * PV)
        if post == "v":
            relu(p * PV, (p + 1) * PV)

    def v_last(key, p, on_a):
        c = p * PV
        for a, b in ((0, 32), (32, 48), (48, 64)):
            x_gather(key, c + a, c + b)
            (absd if on_a else relu)(c + a, c + b)
            score(p, R("scb", 0, PV), a // 4, b // 4, not on_a)

    def tail(t):
        tk, nd = "t%d" % t, ND[t]
        keys, begin = R("sc", 15, V, 16), len(tasks)
        copy(full("ki"), keys)
        ts(full("par"), full("ki"), 1, Op.bitwise_and)
        copy(full("parf"), full("par"))
        mm(R("sca", 0, 24), [(full("ones"), full("parf"))])
        urgent[len(tasks) - 1] = 3
        ts(full("kk"), full("ki"), 15, Op.bitwise_and)
        op("v", lambda: V_.tensor_reduce(ap(col("ss", 0)), ap(R("sca", 0, 24)), AxisListType.X, Op.add),
           [R("sca", 0, 24)], [col("ss", 0)], 64)
        ts(full("tt"), keys, col("ss", 0), Op.add, 1.0, Op.add)
        ts(full("yy"), full("tt"), 15, Op.bitwise_and)
        ts(full("a0"), full("yy"), 1.0, Op.max, 128.0, Op.mult)
        ts(full("ee"), full("yy"), 8.0, Op.is_lt, 2048.0, Op.mult)
        tt(full("o0"), full("a0"), full("qw"), Op.add)
        copy(full("u0"), full("o0"))
        tt(full("o1"), full("o0"), full("ee"), Op.add)
        o = own(tk)
        for z, bank in (("z5", "db"), ("z3", "da")) if t > 1 else ():
            for part in range(3):
                rn2(part, R(bank, 128 * part, 128 * (part + 1)), z)
                turns["rn%d%s%d" % (t, z, part)] = [begin + 3, len(tasks) - 1]
                urgent[len(tasks) - 1] = 0
        ts(full("u1"), full("o1"), -1024.0, Op.add)
        for h in range(TCUT):
            a, b = h * 24 // TCUT, (h + 1) * 24 // TCUT
            gather(R(tk, o[1] + 32 * a, o[1] + 32 * b, 2), full("ww"), R("u0", a, b), "a")
            gather(R(tk, o[1] + 32 * a + 1, o[1] + 32 * b, 2), full("ww"), R("u1", a, b))
        gate = len(tasks) - 1
        for i in range(begin, len(tasks)):
            urgent.setdefault(i, 1)
        send(tk)
        mask_list(t)
        tt(full("ox"), full("c16"), full("kk"), Op.subtract)
        copy(full("oxu"), full("ox"))
        c = nd * PV
        old = own("x%d" % (t - 1))
        nxt = own("x%d" % t) if t < 3 else full("xo")
        if c:
            tt(R("dq", 0, c), full("dd"), R("zz", 0, c), Op.add, off=R("oxu", 0, c // 16))
            copy(R(nxt[0], nxt[1], nxt[1] + c), R("dq", 0, c))
        ts(R("dq", c, V), full("dd"), -1.5, Op.add, 0.25, Op.mult, off=R("oxu", c // 16, V // 16))
        tt(R(nxt[0], nxt[1] + c, nxt[2]), R("dq", c, V), R(old[0], old[1] + c, old[2]), Op.add)
        if t < 3:
            send("x%d" % t)
        else:
            dma("s", T.yx[:], ap(nxt), [nxt], [], "st")
        rest = xrep("x%d" % t, ND[t + 1], 0, XG) if t < 3 else []
        t_list(t)
        for p in range(NP):
            mask(p, MENG[t][p].replace("x", "any"))
        for f in rest:
            f()
        open_t(t)
        if t < 3:
            open_x(t + 1)
        gates[gate] = len(tasks)

    dma("s", ap(own("x0")), T.x[:], [], [own("x0")], "ldx")
    dma("a", ap(full("rin")), T.rot[:], [], [full("rin")], "ldr")
    iota(col("pid", 0), [[0, 1]], 0, 1)
    iota(full("vq0"), [[64, 6], [4, 4]], 0, 0)
    iota(full("ci"), [[1, 144]], -15, 0)
    iota(full("qb0"), [[64, 6], [1, 4]], 0, 0)
    fill(full("ones"), 1.0)
    fill(full("d0"), 1.0)
    perm(1)
    perm(2)
    send("x0")
    for m in range(3, 8):
        perm(m)
    iota(full("qw0"), [[2048, 3], [64, 2], [1, 4]], 0, 0)
    for c, mk in enumerate((0x70, 0x78, 0x77, 7, 8, 3, None, 15)):
        if mk is None:
            ts(col("pi", c), col("pid", 0), 2, Op.logical_shift_right, 3, Op.bitwise_and)
        else:
            ts(col("pi", c), col("pid", 0), mk, Op.bitwise_and)
    fill(R("d0", 0, V, 16), -1.0e6)
    copy(full("pf"), full("pi"))
    copy(col("pc", 5), col("pid", 0))
    ts(col("pc", 0), col("pf", 5), 16.0, Op.mult, col("pf", 6), Op.add)
    ts(col("pc", 1), col("pf", 4), 0.125, Op.mult)
    ts(col("pc", 2), col("pf", 4), -0.125, Op.mult, 1.0, Op.add)
    ts(full("vq"), full("vq0"), col("pc", 0), Op.add)
    ts(R("z40", 0, 136), R("ci", 7, 143), col("pf", 2), Op.is_equal, col("pc", 2), Op.mult)
    ts(R("z41", 0, 136), R("ci", 7, 143), col("pf", 2), Op.is_equal, col("pc", 1), Op.mult)
    gather(full("ri"), full("rin"), full("vq"))
    ts(full("rj"), full("ri"), 8, Op.logical_shift_right)
    ts(full("rk"), full("ri"), 255, Op.bitwise_and)
    copy(full("hi"), full("rj"))
    copy(full("lo"), full("rk"))
    for ih, name in ((0, "ra"), (1, "rb")):
        z = "z4%d" % ih
        mm(R(name, 0, V), [(R(z, 8, 136), full("hi")), (R(z, 0, 128), full("lo"))])
        for part in range(3):
            copy(wat(part, 8 * ih, 8 * ih + 1), R(name, 128 * part, 128 * (part + 1)), "a")
    ts(full("far"), full("ri"), -7.5, Op.add, 0.0625, Op.mult)
    for z, w in (("e4", 4.0), ("en", -1.0), ("e0", 0.0)):
        ts(full(z), R("ci", 15, 143), col("pc", 5), Op.is_equal, w, Op.mult)
    for f in xrep("x0", ND[1], 0, XG0):
        f()
    open_x(1)
    for part in range(3):
        w_half(part, 0, "any")
        w_half(part, 1, "any")
    for z, w in (("zs", 16.0), ("zp", 32.0), ("zn", -16.0)):
        ts(R(z, 0, 143), R("ci", 0, 143), col("pf", 0), Op.is_equal, w, Op.mult)
    ts(col("pc", 3), col("pf", 7), 4.0, Op.mult)
    ts(col("pc", 4), col("pf", 4), -31.875, Op.mult, 256.0, Op.add)
    iota(full("em0"), [[0, 32], [1, 8]], 0, 0)
    ts(full("em"), full("em0"), col("pf", 3), Op.is_equal)
    ts(full("qb"), full("qb0"), col("pc", 3), Op.add)
    ts(full("qw"), full("qw0"), col("pc", 3), Op.add)
    ts(full("c16"), full("qb"), 16.0, Op.mult, 15.0, Op.add)
    copy(full("qv"), full("qb"))
    ts(col("pj", 0), col("pid", 0), 3, Op.logical_shift_right)
    ts(col("pj", 1), col("pid", 0), 4, Op.logical_shift_right)
    ts(col("pc", 7), col("pj", 1), col("pf", 4), Op.add)
    copy(col("pc", 6), col("pj", 0))
    ts(full("z6"), R("ci", 15, 31), col("pc", 6), Op.is_equal)
    ts(full("z7"), R("ci", 15, 31), col("pc", 7), Op.is_equal)
    ts(R("z5", 0, 136), R("ci", 7, 143), col("pf", 2), Op.is_equal, col("pc", 1), Op.mult)
    ts(R("zr", 0, 143), R("ci", 0, 143), col("pf", 0), Op.is_equal, col("pc", 4), Op.mult)
    ts(R("z3", 0, 136), R("ci", 7, 143), col("pf", 2), Op.is_equal, col("pc", 4), Op.mult)
    ts(R("z2", 0, 135), R("ci", 8, 143), col("pf", 1), Op.is_equal)
    for z, w in (("e1", 1.0), ("e256", 256.0)):
        ts(full(z), R("ci", 15, 143), col("pc", 5), Op.is_equal, w, Op.mult)

    def x_phase(t):
        key, nd = "x%d" % (t - 1), ND[t]
        for p in XORD[t]:
            bank = R("ra", 0, PV) if p == nd - 1 and XORD[t].index(p) > 3 else R("scb", 0, PV) if p == NP - 1 else R("sca", p * PV, (p + 1) * PV)
            if p < nd:
                s_piece("x", key, p, XB[p])
                score(p, bank)
            elif p == NP - 1:
                v_last(key, p, p in ABS[t])
            else:
                x_gather(key, p * PV, (p + 1) * PV)
                (absd if p in ABS[t] else relu)(p * PV, (p + 1) * PV)
                score(p, bank, from_relu=p not in ABS[t])
            scan(p, p + 1, bank)

    def t_piece(t, p):
        banks = t_banks(t, p)
        s_piece("t", "t%d" % t, p, banks)
        mine = [chunk(p, h) for h in (0, 1) if h not in banks]
        if mine:
            t_gather("t%d" % t, mine[0][0], mine[-1][1])

    x_phase(1)
    tail(1)

    for t in (2, 3):
        fars = []
        for p in range(NP):
            t_piece(t - 1, p)
            begin = len(tasks)
            if p // 2 not in STAT:
                r2(p)
            if p % 2:
                (r2s if p // 2 in STAT else r2copy)(p // 2)
                rn2(p // 2)
                far(p // 2)
                fars.append(len(tasks) - 1)
            urgent.update((i, FU) for i in range(begin, len(tasks)))
        if FAR0:
            turns["far%d" % t] = [last_t[FAR0], fars[0]]
        del last_t[:]
        x_phase(t)
        last_abs = max(i for i, x in enumerate(tasks) if x[0] == "a")
        for n in range(6):
            w_half(n // 2, n % 2, WENG[n].replace("x", "any"))
            if n == WLATE:
                turns["w%d" % t] = [last_abs, len(tasks) - 2]
        tail(t)

    def finish(p):
        bank = R(("ra", "scb")[p % 2], 0, PV)
        rn(bank, p * PV, (p + 1) * PV)
        copy(R("rs", p * PV, (p + 1) * PV), bank, "any" if p == NP - 1 else "a")

    def store(p0, p1):
        a, b = p0 * PV, p1 * PV
        dma("s", T.yr[:, a:b], ap(R("rs", a, b)), [R("rs", a, b)], [], "st")

    for p in range(NP):
        t_piece(3, p)
        if p // 2 not in STAT3:
            finish(p)
        elif p % 2:
            name, c = sums(p // 2, "z7", lambda i: (i, 256, 16))
            mm(R(name, 256, 384), [(R("aa", c, c + 128), full("e256")), (R("aa", c + 128, c + 256), full("e1"))])
            copy(R("rs", (p - 1) * PV, (p + 1) * PV), R(name, 256, 384), "a")
        if p in (3, 5):
            store(0 if p == 3 else 4, p + 1)
    if not ORDER:
        ORDER.extend(order())
    for i, e in ORDER:
        issue(*[t for t in [tasks[i]] + other.get(i, []) if t[0] == e][0])
    g.sync.wait_ge(T.sem.st, count["st"])
    g.wait_ge(T.sem.sent, sent[0])
    for s in ("sv", "sa", "sp", "sg"):
        g.wait_ge(T.sem[s], count[s])
